import numpy as np
import ml_dtypes


def mxq(x, axis, fmt="e4m3"):
    dtype, down = {"e4m3": (ml_dtypes.float8_e4m3fn, 7), "e5m2": (ml_dtypes.float8_e5m2, 14)}[fmt]
    v = np.moveaxis(np.asarray(x, np.float32).astype(ml_dtypes.bfloat16).astype(np.float64), axis, -1)
    blocks = v.reshape(v.shape[:-1] + (-1, 32))
    amax = np.abs(blocks).max(-1, keepdims=True)
    byte = np.maximum(np.where(amax > 0, np.frexp(amax)[1] - 1 + 127, 0) - down, 1)
    scale = np.exp2(byte - 127.0)
    codes = (blocks / scale).astype(np.float32).astype(dtype).astype(np.float64)
    return np.moveaxis((codes * scale).reshape(v.shape), -1, axis)


WIDE = False


def mx_kscale(k):
    if not WIDE:
        return np.ones(k)
    levels = np.array([24, -24, 12, -12, 0])
    if k % 512:
        return np.exp2(np.random.permutation(np.resize(levels, k // 32))).repeat(32)
    a = np.empty((k // 512, 16))
    for p in range(k // 512):
        a[p, :8] = np.random.permutation(np.resize(levels, 8))
        for g in range(8):
            far = levels[np.abs(levels - a[p, g]) >= 10]
            a[p, g + 8] = far[np.random.randint(len(far))]
    return np.exp2(a.ravel()).repeat(32)


def f64(x):
    return np.asarray(x).astype(np.float64)


def striped8(idx):
    return np.concatenate([v.reshape(-1, 16).T for v in idx]).astype(np.uint16)


def unstriped8(offs):
    return np.stack([offs[16 * g:16 * g + 16].T.reshape(-1) for g in range(8)]).astype(np.int64)


E2M1 = np.array([0.0, 0.5, 1.0, 1.5, 2.0, 3.0, 4.0, 6.0, -0.0, -0.5, -1.0, -1.5, -2.0, -3.0, -4.0, -6.0])


def pack_weight(w, fmt):
    k, n = w.shape
    w = f64(np.asarray(w, np.float32).astype(ml_dtypes.bfloat16)).reshape(k // 32, 32, n)
    amax = np.abs(w).max(1)
    if fmt == "e4m3":
        byte = np.frexp(amax)[1] - 1 + 127 - 7
    else:
        mant, ex = np.frexp(amax / 6.0)
        byte = np.where(mant > 0.5, ex, ex - 1) + 127
    byte = np.clip(np.where(amax > 0, byte, 1), 1, 254)
    scaled = (w * np.exp2(127.0 - byte)[:, None, :]).reshape(k, n).astype(np.float32)
    by_word = np.ascontiguousarray(scaled.reshape(k // 512, 128, 4, n).transpose(0, 1, 3, 2))
    if fmt == "e4m3":
        words = by_word.astype(ml_dtypes.float8_e4m3fn).view(np.uint8)
    else:
        c = by_word.astype(ml_dtypes.float4_e2m1fn).view(np.uint8) & 0xF
        words = (c[..., 0::2] | (c[..., 1::2] << 4)).reshape(k // 512, 128, 2 * n)
    return np.ascontiguousarray(words), np.ascontiguousarray(byte.astype(np.uint8).reshape(k // 512, 16, n))


def unpack_weight(words, scales, fmt):
    g, _, n = scales.shape
    words = np.ascontiguousarray(words).reshape(g, 128, n, -1)
    if fmt == "e4m3":
        vals = words.view(ml_dtypes.float8_e4m3fn).astype(np.float64)
    else:
        nib = np.empty((g, 128, n, 4), np.uint8)
        nib[..., 0::2] = words & 0xF
        nib[..., 1::2] = words >> 4
        vals = E2M1[nib]
    vals = vals * np.repeat(np.exp2(scales.astype(np.float64) - 127.0), 8, axis=1)[..., None]
    return vals.transpose(0, 1, 3, 2).reshape(g * 512, n)


def sigm(f):
    return 1.0 / (1.0 + np.exp(-np.maximum(f, -700.0)))


K, N, T, J = 1024, 512, 2048, 1024


def setup_inputs():
    n = np.random.standard_normal
    s = mx_kscale(K)[:, None]
    p_wk = pack_weight(n((K, N)) / np.sqrt(K) / s, "e2m1")
    return {
        "xT": (n((K, T)) * s).astype(np.float32),
        "wgt": np.repeat(np.random.uniform(0.5, 2.0, (8, J)), 16, axis=0).astype(np.float32),
        "wk_words": p_wk[0],
        "wk_scales": p_wk[1],
        "wv": (n((K, N)) / np.sqrt(K) / s).astype(np.float32),
        "bg": (0.3 * n(N) - 1.0).astype(np.float32),
        "res": (n((N, J))).astype(np.float32),
        "offs": striped8(np.stack([np.random.permutation(T)[:J] for _ in range(8)])),
    }


def reference(xT, wgt, wk_words, wk_scales, wv, bg, res, offs):
    idx = unstriped8(offs)
    rows = np.arange(K)
    xg = f64(wgt)[rows // 4 % 128] * f64(xT)[rows[:, None], idx[rows % 512 // 64]]
    xT_ = mxq(xg, 0, "e4m3")
    wk_ = unpack_weight(wk_words, wk_scales, "e2m1")
    wv_ = mxq(f64(wv), 0, "e4m3")
    ke = wk_.T @ xT_
    ve = wv_.T @ xT_
    gate = sigm(ke + f64(bg)[:, None])
    return f64(res) + gate * (ve - f64(res))

@@ -1,0 +1,220 @@
+from contextlib import ExitStack
+
+import concourse.mybir as mybir
+
+K, N, T, J = 1024, 512, 2048, 1024
+FLOPS = 2 * 2 * K * N * J
+
+F32 = mybir.dt.float32
+BF16 = mybir.dt.bfloat16
+I32 = mybir.dt.int32
+U32 = mybir.dt.uint32
+U16 = mybir.dt.uint16
+U8 = mybir.dt.uint8
+FP8X4 = mybir.dt.float8_e4m3fn_x4
+FP4X4 = mybir.dt.float4_e2m1fn_x4
+ALU = mybir.AluOpType
+ACT = mybir.ActivationFunctionType
+
+P = 128
+PACK = 4
+K_PASS = P * PACK
+PASSES = K // K_PASS
+JH = 512
+HALVES = J // JH
+NH = 256
+N_TILES = N // P
+
+
+def tile_list_hway_kernel(tc, xT, wgt, wk_words, wk_scales, wv, bg, res, offs, out):
+    nc = tc.nc
+    with ExitStack() as ctx:
+        keep = ctx.enter_context(tc.tile_pool(name="keep", bufs=1))
+        work = ctx.enter_context(tc.tile_pool(name="work", bufs=4))
+        psum = ctx.enter_context(tc.psum_pool(name="psum", bufs=4))
+
+        offsets = keep.tile([P, J // 16], U16, name="offsets")
+        weights = [keep.tile([P, JH], F32, name="weights%d" % h) for h in range(HALVES)]
+        planes = [[keep.tile([P, T], F32, name="plane%d_%d" % (a, i)) for i in range(PACK)] for a in range(PASSES)]
+        wk_codes = keep.tile([P, PASSES, 2 * N], U8, name="wk_codes", align_bytes=64)
+        wk_plane = keep.tile([P, PASSES, N], U8, name="wk_plane", align_bytes=64)
+        bias = keep.tile([P, N_TILES], F32, name="bias")
+        wv_raw = [[keep.tile([P, PACK, NH], F32, name="wv_raw%d_%d" % (a, m)) for m in range(2)] for a in range(PASSES)]
+        res_sb = [keep.tile([P, 2, J], F32, name="res%d" % m) for m in range(2)]
+        warm = keep.tile([P, 8], F32, name="warm")
+        warm2 = keep.tile([P, 8], F32, name="warm2")
+
+        nc.vector.memset(warm[:], 0.0)
+        nc.scalar.activation(warm2[:], warm[:], ACT.Sigmoid)
+        nc.vector.memset(wk_plane[:].rearrange("p a n -> p (a n)").bitcast(I32), 0)
+
+        def load_plane(a, i):
+            rows = xT[a * K_PASS:(a + 1) * K_PASS, :].rearrange("(p i) t -> p i t", i=PACK)
+            nc.sync.dma_start(planes[a][i][:], rows[:, i, :])
+
+        def load_wv(a, m):
+            rows = wv[a * K_PASS:(a + 1) * K_PASS, :].rearrange("(p i) n -> p i n", i=PACK)
+            nc.sync.dma_start(wv_raw[a][m][:], rows[:, :, m * NH:(m + 1) * NH])
+
+        def load_res(nt):
+            nc.sync.dma_start(res_sb[nt // 2][:, nt % 2, :], res[nt * P:(nt + 1) * P, :])
+
+        nc.sync.dma_start(offsets[:], offs)
+        nc.sync.dma_start(weights[0][:], wgt[:, 0:JH])
+        load_plane(0, 0)
+        nc.sync.dma_start(weights[1][:], wgt[:, JH:J])
+        load_plane(0, 1)
+        load_plane(0, 2)
+        load_plane(0, 3)
+        for q in range(4):
+            nc.sync.dma_start(
+                wk_plane[32 * q:32 * q + 4, :, :].bitcast(I32),
+                wk_scales[:, 4 * q:4 * q + 4, :].rearrange("a r n -> r a n").bitcast(I32),
+            )
+        with nc.allow_non_contiguous_dma(reason="one bias value for each partition"):
+            nc.sync.dma_start(bias[:], bg.rearrange("(c p) -> p c", p=P))
+        nc.sync.dma_start(wk_codes[:].bitcast(I32), wk_words.rearrange("a p b -> p a b").bitcast(I32))
+        load_plane(1, 0)
+        load_wv(0, 0)
+        load_plane(1, 1)
+        load_wv(1, 0)
+        load_plane(1, 2)
+        load_plane(1, 3)
+        load_res(0)
+        load_res(1)
+        load_wv(0, 1)
+        load_wv(1, 1)
+        load_res(2)
+        load_res(3)
+
+        def interleave(name, src, width):
+            grouped = keep.tile([P, width, PACK], BF16, name=name + "_bf", align_bytes=64)
+            nc.scalar.copy(
+                grouped[:].rearrange("p (c r) i -> p c i r", r=4),
+                src.rearrange("p i (c r) -> p c i r", r=4),
+            )
+            return grouped
+
+        def operand(name, width):
+            codes = keep.tile([P, width], U32, name=name + "_codes", align_bytes=64)
+            scales = keep.tile([P, width], U8, name=name + "_scales", align_bytes=64)
+            return codes, scales
+
+        def quantize(target, c0, grouped, width):
+            codes, scales = target
+            nc.vector.quantize_mx(codes[:, c0:c0 + width].bitcast(FP8X4), scales[:, c0:c0 + width],
+                                  grouped[:].rearrange("p w i -> p (w i)"))
+
+        picked = [[keep.tile([P, PACK, JH], F32, name="picked%d_%d" % (a, h)) for h in range(HALVES)] for a in range(PASSES)]
+        xq = [[operand("xg%d_%d" % (a, h), JH) for h in range(HALVES)] for a in range(PASSES)]
+        vq = [[operand("wv%d_%d" % (a, m), NH) for m in range(2)] for a in range(PASSES)]
+
+        def gather(a, i, j0, width):
+            h, c0 = divmod(j0, JH)
+            nc.vector.tensor_tensor(
+                picked[a][h][:, i, c0:c0 + width],
+                planes[a][i][:].indirect(offsets[:, j0 // 16:(j0 + width) // 16]),
+                weights[h][:, c0:c0 + width],
+                ALU.mult,
+            )
+
+        def make_xq(a, j0, width):
+            h, c0 = divmod(j0, JH)
+            grouped = interleave("xg%d_%d" % (a, j0), picked[a][h][:, :, c0:c0 + width], width)
+            quantize(xq[a][h], c0, grouped, width)
+
+        def make_vq(a, m):
+            quantize(vq[a][m], 0, interleave("wv%d_%d" % (a, m), wv_raw[a][m][:], NH), NH)
+
+        banks = {}
+
+        def multiply(unit, a):
+            nt0, count, j0, width = unit
+            if a == 0:
+                ke = psum.tile([P, count, width], F32, name="ke")
+                ve = psum.tile([P, count, width], F32, name="ve")
+                banks[unit] = (ke, ve)
+            ke, ve = banks[unit]
+            h, c0 = divmod(j0, JH)
+            codes, scales = xq[a][h]
+            for u in range(count):
+                nt = nt0 + u
+                v_codes, v_scales = vq[a][nt // 2]
+                v0 = (nt % 2) * P
+                nc.tensor.matmul_mx(
+                    ve[:, u, :], lhsT=v_codes[:, v0:v0 + P].bitcast(FP8X4), lhsT_scale=v_scales[:, v0:v0 + P],
+                    rhs=codes[:, c0:c0 + width].bitcast(FP8X4), rhs_scale=scales[:, c0:c0 + width],
+                    start=(a == 0 and u == 0), stop=(a == PASSES - 1 and u == count - 1))
+            step = width if width == JH else P
+            for u in range(count):
+                nt = nt0 + u
+                for b in range(0, width, step):
+                    nc.tensor.matmul_mx(
+                        ke[:, u, b:b + step], lhsT=wk_codes[:, a, 2 * P * nt:2 * P * (nt + 1)].bitcast(FP4X4),
+                        lhsT_scale=wk_plane[:, a, P * nt:P * (nt + 1)],
+                        rhs=codes[:, c0 + b:c0 + b + step].bitcast(FP8X4), rhs_scale=scales[:, c0 + b:c0 + b + step],
+                        start=(a == 0 and u == 0 and b == 0),
+                        stop=(a == PASSES - 1 and u == count - 1 and b + step == width))
+
+        def res_of(unit):
+            nt0, count, j0, width = unit
+            return res_sb[nt0 // 2][:, nt0 % 2:nt0 % 2 + count, j0:j0 + width]
+
+        def finish(pair):
+            gates = []
+            diffs = []
+            for unit in pair:
+                nt0, count, j0, width = unit
+                ke, ve = banks[unit]
+                gate = work.tile([P, count, width], F32, name="gate")
+                for u in range(count):
+                    nc.scalar.activation(gate[:, u, :], ke[:, u, :], ACT.Sigmoid, bias=bias[:, nt0 + u:nt0 + u + 1])
+                diff = work.tile([P, count, width], F32, name="diff")
+                nc.vector.tensor_tensor(diff[:], ve[:], res_of(unit), ALU.subtract)
+                gates.append(gate)
+                diffs.append(diff)
+            for gate, diff in zip(gates, diffs):
+                nc.vector.tensor_tensor(diff[:], diff[:], gate[:], ALU.mult)
+            for unit, diff in zip(pair, diffs):
+                nt0, count, j0, width = unit
+                result = work.tile([P, count, width], F32, name="result")
+                nc.vector.tensor_tensor(result[:], diff[:], res_of(unit), ALU.add)
+                rows = out[nt0 * P:(nt0 + count) * P, j0:j0 + width].rearrange("(u p) j -> p u j", p=P)
+                nc.sync.dma_start(rows, result[:])
+
+        JQ = JH // 2
+        first = [(0, 2, 0, JQ), (0, 2, JQ, JQ), (0, 1, JH, JH), (1, 1, JH, JH)]
+        later = [(2, 1, 0, JH), (3, 1, 0, JH), (2, 1, JH, JH), (3, 1, JH, JH)]
+
+        for i in range(PACK):
+            for h in range(HALVES):
+                gather(0, i, h * JH, JH)
+        for h in range(HALVES):
+            make_xq(0, h * JH, JH)
+        make_vq(0, 0)
+        for unit in first:
+            multiply(unit, 0)
+        make_vq(1, 0)
+        for i in range(PACK - 1):
+            for h in range(HALVES):
+                gather(1, i, h * JH, JH)
+        gather(1, PACK - 1, 0, JQ)
+        gather(1, PACK - 1, JQ, JQ)
+        gather(1, PACK - 1, JH, JH)
+        make_xq(1, 0, JQ)
+        multiply(first[0], 1)
+        make_xq(1, JQ, JQ)
+        multiply(first[1], 1)
+        make_xq(1, JH, JQ)
+        finish(first[0:2])
+        make_xq(1, JH + JQ, JQ)
+        multiply(first[2], 1)
+        multiply(first[3], 1)
+        make_vq(0, 1)
+        make_vq(1, 1)
+        finish(first[2:4])
+        for unit in later:
+            multiply(unit, 0)
+            multiply(unit, 1)
+        finish(later[0:2])
+        finish(later[2:4])

@@ -1,6 +1,7 @@
 from contextlib import ExitStack
 
 import concourse.mybir as mybir
+from concourse.masks import make_identity
 
 K, N, T, J = 1024, 512, 2048, 1024
 FLOPS = 2 * 2 * K * N * J
@@ -34,16 +35,22 @@ def tile_list_hway_kernel(tc, xT, wgt, wk_words, wk_scales, wv, bg, res, offs, o
         psum = ctx.enter_context(tc.psum_pool(name="psum", bufs=4))
 
         offsets = keep.tile([P, J // 16], U16, name="offsets")
-        weights = [keep.tile([P, JH], F32, name="weights%d" % h) for h in range(HALVES)]
-        planes = [[keep.tile([P, T], F32, name="plane%d_%d" % (a, i)) for i in range(PACK)] for a in range(PASSES)]
+        weights = keep.tile([P, J], F32, name="weights")
+        planes = [[keep.tile([P, T], F32, name="plane%d_%d" % (a, i), tag="plane%d_%d" % (a, i), align_bytes=64)
+                   for i in range(PACK)] for a in range(PASSES)]
         wk_codes = keep.tile([P, PASSES, 2 * N], U8, name="wk_codes", align_bytes=64)
         wk_plane = keep.tile([P, PASSES, N], U8, name="wk_plane", align_bytes=64)
         bias = keep.tile([P, N_TILES], F32, name="bias")
         wv_raw = [[keep.tile([P, PACK, NH], F32, name="wv_raw%d_%d" % (a, m)) for m in range(2)] for a in range(PASSES)]
+        wv_bf = [keep.tile([P, PASSES, NH, PACK], BF16, name="wv_bf%d" % m, align_bytes=64) for m in range(2)]
         res_sb = [keep.tile([P, 2, J], F32, name="res%d" % m) for m in range(2)]
         warm = keep.tile([P, 8], F32, name="warm")
         warm2 = keep.tile([P, 8], F32, name="warm2")
 
+        bias_rows = keep.tile([P, P], F32, name="bias_rows")
+        identity = keep.tile([P, P], F32, name="identity")
+        make_identity(nc, identity[:])
+        nc.vector.memset(bias_rows[:], 0.0)
         nc.vector.memset(warm[:], 0.0)
         nc.scalar.activation(warm2[:], warm[:], ACT.Sigmoid)
         nc.vector.memset(wk_plane[:].rearrange("p a n -> p (a n)").bitcast(I32), 0)
@@ -60,9 +67,9 @@ def tile_list_hway_kernel(tc, xT, wgt, wk_words, wk_scales, wv, bg, res, offs, o
             nc.sync.dma_start(res_sb[nt // 2][:, nt % 2, :], res[nt * P:(nt + 1) * P, :])
 
         nc.sync.dma_start(offsets[:], offs)
-        nc.sync.dma_start(weights[0][:], wgt[:, 0:JH])
+        nc.sync.dma_start(weights[:, 0:JH], wgt[:, 0:JH])
         load_plane(0, 0)
-        nc.sync.dma_start(weights[1][:], wgt[:, JH:J])
+        nc.sync.dma_start(weights[:, JH:J], wgt[:, JH:J])
         load_plane(0, 1)
         load_plane(0, 2)
         load_plane(0, 3)
@@ -71,60 +78,61 @@ def tile_list_hway_kernel(tc, xT, wgt, wk_words, wk_scales, wv, bg, res, offs, o
                 wk_plane[32 * q:32 * q + 4, :, :].bitcast(I32),
                 wk_scales[:, 4 * q:4 * q + 4, :].rearrange("a r n -> r a n").bitcast(I32),
             )
-        with nc.allow_non_contiguous_dma(reason="one bias value for each partition"):
-            nc.sync.dma_start(bias[:], bg.rearrange("(c p) -> p c", p=P))
-        nc.sync.dma_start(wk_codes[:].bitcast(I32), wk_words.rearrange("a p b -> p a b").bitcast(I32))
+        nc.sync.dma_start(bias_rows[0:N_TILES, :], bg.rearrange("(c p) -> c p", p=P))
         load_plane(1, 0)
-        load_wv(0, 0)
         load_plane(1, 1)
-        load_wv(1, 0)
+        load_wv(0, 0)
         load_plane(1, 2)
+        load_wv(1, 0)
+        nc.sync.dma_start(wk_codes[:].bitcast(I32), wk_words.rearrange("a p b -> p a b").bitcast(I32))
         load_plane(1, 3)
         load_res(0)
         load_res(1)
+        load_res(2)
         load_wv(0, 1)
         load_wv(1, 1)
-        load_res(2)
         load_res(3)
 
-        def interleave(name, src, width):
-            grouped = keep.tile([P, width, PACK], BF16, name=name + "_bf", align_bytes=64)
+        bias_turned = psum.tile([P, P], F32, name="ke")
+        nc.tensor.transpose(bias_turned[:], bias_rows[:], identity[:])
+        nc.scalar.copy(bias[:], bias_turned[:, 0:N_TILES])
+
+        def interleave(grouped, src):
             nc.scalar.copy(
-                grouped[:].rearrange("p (c r) i -> p c i r", r=4),
+                grouped.rearrange("p (c r) i -> p c i r", r=4),
                 src.rearrange("p i (c r) -> p c i r", r=4),
             )
-            return grouped
 
-        def operand(name, width):
-            codes = keep.tile([P, width], U32, name=name + "_codes", align_bytes=64)
+        def operand(name, width, tag):
+            codes = keep.tile([P, width], U32, name=name + "_codes", tag=tag, align_bytes=64)
             scales = keep.tile([P, width], U8, name=name + "_scales", align_bytes=64)
             return codes, scales
 
-        def quantize(target, c0, grouped, width):
-            codes, scales = target
-            nc.vector.quantize_mx(codes[:, c0:c0 + width].bitcast(FP8X4), scales[:, c0:c0 + width],
-                                  grouped[:].rearrange("p w i -> p (w i)"))
-
-        picked = [[keep.tile([P, PACK, JH], F32, name="picked%d_%d" % (a, h)) for h in range(HALVES)] for a in range(PASSES)]
-        xq = [[operand("xg%d_%d" % (a, h), JH) for h in range(HALVES)] for a in range(PASSES)]
-        vq = [[operand("wv%d_%d" % (a, m), NH) for m in range(2)] for a in range(PASSES)]
+        picked = [keep.tile([P, PACK, J], F32, name="picked%d" % a) for a in range(PASSES)]
+        xq = {}
+        vq = {}
 
         def gather(a, i, j0, width):
-            h, c0 = divmod(j0, JH)
             nc.vector.tensor_tensor(
-                picked[a][h][:, i, c0:c0 + width],
+                picked[a][:, i, j0:j0 + width],
                 planes[a][i][:].indirect(offsets[:, j0 // 16:(j0 + width) // 16]),
-                weights[h][:, c0:c0 + width],
+                weights[:, j0:j0 + width],
                 ALU.mult,
             )
 
         def make_xq(a, j0, width):
-            h, c0 = divmod(j0, JH)
-            grouped = interleave("xg%d_%d" % (a, j0), picked[a][h][:, :, c0:c0 + width], width)
-            quantize(xq[a][h], c0, grouped, width)
+            grouped = keep.tile([P, width, PACK], BF16, name="xg_bf%d_%d" % (a, j0), align_bytes=64)
+            interleave(grouped[:], picked[a][:, :, j0:j0 + width])
+            codes, scales = xq[a, j0 // JH]
+            c0 = j0 % JH
+            nc.vector.quantize_mx(codes[:, c0:c0 + width].bitcast(FP8X4), scales[:, c0:c0 + width],
+                                  grouped[:].rearrange("p w i -> p (w i)"))
 
-        def make_vq(a, m):
-            quantize(vq[a][m], 0, interleave("wv%d_%d" % (a, m), wv_raw[a][m][:], NH), NH)
+        def make_vq(m):
+            for a in range(PASSES):
+                interleave(wv_bf[m][:, a, :, :], wv_raw[a][m][:])
+            codes, scales = vq[m]
+            nc.vector.quantize_mx(codes.bitcast(FP8X4), scales, wv_bf[m][:].rearrange("p a w i -> p (a w i)"))
 
         banks = {}
 
@@ -135,12 +143,12 @@ def tile_list_hway_kernel(tc, xT, wgt, wk_words, wk_scales, wv, bg, res, offs, o
                 ve = psum.tile([P, count, width], F32, name="ve")
                 banks[unit] = (ke, ve)
             ke, ve = banks[unit]
-            h, c0 = divmod(j0, JH)
-            codes, scales = xq[a][h]
+            c0 = j0 % JH
+            codes, scales = xq[a, j0 // JH]
             for u in range(count):
                 nt = nt0 + u
-                v_codes, v_scales = vq[a][nt // 2]
-                v0 = (nt % 2) * P
+                v_codes, v_scales = vq[nt // 2]
+                v0 = a * NH + (nt % 2) * P
                 nc.tensor.matmul_mx(
                     ve[:, u, :], lhsT=v_codes[:, v0:v0 + P].bitcast(FP8X4), lhsT_scale=v_scales[:, v0:v0 + P],
                     rhs=codes[:, c0:c0 + width].bitcast(FP8X4), rhs_scale=scales[:, c0:c0 + width],
@@ -178,26 +186,37 @@ def tile_list_hway_kernel(tc, xT, wgt, wk_words, wk_scales, wv, bg, res, offs, o
             for unit, diff in zip(pair, diffs):
                 nt0, count, j0, width = unit
                 result = work.tile([P, count, width], F32, name="result")
-                nc.vector.tensor_tensor(result[:], diff[:], res_of(unit), ALU.add)
                 rows = out[nt0 * P:(nt0 + count) * P, j0:j0 + width].rearrange("(u p) j -> p u j", p=P)
-                nc.sync.dma_start(rows, result[:])
+                step = width // 2 if unit == later[-1] else width
+                for b in range(0, width, step):
+                    nc.vector.tensor_tensor(result[:, :, b:b + step], diff[:, :, b:b + step],
+                                            res_of(unit)[:, :, b:b + step], ALU.add)
+                    nc.sync.dma_start(rows[:, :, b:b + step], result[:, :, b:b + step])
 
         JQ = JH // 2
         first = [(0, 2, 0, JQ), (0, 2, JQ, JQ), (0, 1, JH, JH), (1, 1, JH, JH)]
         later = [(2, 1, 0, JH), (3, 1, 0, JH), (2, 1, JH, JH), (3, 1, JH, JH)]
 
-        for i in range(PACK):
-            for h in range(HALVES):
-                gather(0, i, h * JH, JH)
-        for h in range(HALVES):
-            make_xq(0, h * JH, JH)
-        make_vq(0, 0)
+        gather(0, 0, 0, JH)
+        gather(0, 0, JH, JH)
+        for i in range(1, PACK):
+            gather(0, i, 0, J)
+        gather(1, 0, 0, J)
+        gather(1, 1, 0, J)
+        xq[0, 0] = operand("xg0_0", JH, "plane1_1")
+        make_xq(0, 0, JH)
+        gather(1, 2, 0, J)
+        both = operand("behind6", 2 * JH, "plane1_2")
+        vq[0] = (both[0][:, 0:JH], both[1][:, 0:JH])
+        xq[0, 1] = (both[0][:, JH:J], both[1][:, JH:J])
+        make_vq(0)
+        make_xq(0, JH, JH)
         for unit in first:
             multiply(unit, 0)
-        make_vq(1, 0)
-        for i in range(PACK - 1):
-            for h in range(HALVES):
-                gather(1, i, h * JH, JH)
+        for h in range(HALVES):
+            xq[1, h] = operand("xg1_%d" % h, JH, "xg1_%d" % h)
+        later_v = operand("wv1", JH, "wv1")
+        vq[1] = (later_v[0][:], later_v[1][:])
         gather(1, PACK - 1, 0, JQ)
         gather(1, PACK - 1, JQ, JQ)
         gather(1, PACK - 1, JH, JH)
@@ -210,8 +229,7 @@ def tile_list_hway_kernel(tc, xT, wgt, wk_words, wk_scales, wv, bg, res, offs, o
         make_xq(1, JH + JQ, JQ)
         multiply(first[2], 1)
         multiply(first[3], 1)
-        make_vq(0, 1)
-        make_vq(1, 1)
+        make_vq(1)
         finish(first[2:4])
         for unit in later:
             multiply(unit, 0)

@@ -31,11 +31,11 @@ def tile_list_hway_kernel(tc, xT, wgt, wk_words, wk_scales, wv, bg, res, offs, o
     nc = tc.nc
     with ExitStack() as ctx:
         keep = ctx.enter_context(tc.tile_pool(name="keep", bufs=1))
-        work = ctx.enter_context(tc.tile_pool(name="work", bufs=4))
+        work = ctx.enter_context(tc.tile_pool(name="work", bufs=3))
         psum = ctx.enter_context(tc.psum_pool(name="psum", bufs=4))
 
         offsets = keep.tile([P, J // 16], U16, name="offsets")
-        weights = keep.tile([P, J], F32, name="weights")
+        weights = keep.tile([P, J], F32, name="weights", align_bytes=64)
         planes = [[keep.tile([P, T], F32, name="plane%d_%d" % (a, i), tag="plane%d_%d" % (a, i), align_bytes=64)
                    for i in range(PACK)] for a in range(PASSES)]
         wk_codes = keep.tile([P, PASSES, 2 * N], U8, name="wk_codes", align_bytes=64)
@@ -43,7 +43,7 @@ def tile_list_hway_kernel(tc, xT, wgt, wk_words, wk_scales, wv, bg, res, offs, o
         bias = keep.tile([P, N_TILES], F32, name="bias")
         wv_raw = [[keep.tile([P, PACK, NH], F32, name="wv_raw%d_%d" % (a, m)) for m in range(2)] for a in range(PASSES)]
         wv_bf = [keep.tile([P, PASSES, NH, PACK], BF16, name="wv_bf%d" % m, align_bytes=64) for m in range(2)]
-        res_sb = [keep.tile([P, 2, J], F32, name="res%d" % m) for m in range(2)]
+        res_sb = {(m, h): keep.tile([P, 2, JH], F32, name="res%d_%d" % (m, h)) for m in range(2) for h in range(HALVES)}
         warm = keep.tile([P, 8], F32, name="warm")
         warm2 = keep.tile([P, 8], F32, name="warm2")
 
@@ -63,13 +63,30 @@ def tile_list_hway_kernel(tc, xT, wgt, wk_words, wk_scales, wv, bg, res, offs, o
             rows = wv[a * K_PASS:(a + 1) * K_PASS, :].rearrange("(p i) n -> p i n", i=PACK)
             nc.sync.dma_start(wv_raw[a][m][:], rows[:, :, m * NH:(m + 1) * NH])
 
-        def load_res(nt):
-            nc.sync.dma_start(res_sb[nt // 2][:, nt % 2, :], res[nt * P:(nt + 1) * P, :])
+        def block_of(matrix, m, h):
+            return matrix[m * NH:(m + 1) * NH, h * JH:(h + 1) * JH].rearrange("(u p) j -> p u j", p=P)
 
-        nc.sync.dma_start(offsets[:], offs)
-        nc.sync.dma_start(weights[:, 0:JH], wgt[:, 0:JH])
+        def load_res(m, h):
+            nc.sync.dma_start(res_sb[m, h][:], block_of(res, m, h))
+
+        w_rows = keep.tile([P, 2, 32], F32, name="w_rows", align_bytes=64)
+        w_turned = keep.tile([P, 2, 32], F32, name="w_turned", align_bytes=64)
+        w_spread = keep.tile([P, 32, 2, 16], F32, name="w_spread", align_bytes=64)
+        for q in range(4):
+            nc.sync.dma_start(w_rows[32 * q:32 * q + 32, :, :],
+                            wgt[32 * q:32 * q + 32:16, :].rearrange("g (b s) -> b g s", s=32))
         load_plane(0, 0)
-        nc.sync.dma_start(weights[:, JH:J], wgt[:, JH:J])
+        nc.sync.dma_start(offsets[:], offs)
+        for g in range(2):
+            nc.vector.transpose(w_turned[:, g, :], w_rows[:, g, :])
+        for h in range(HALVES):
+            blocks = slice(16 * h, 16 * (h + 1))
+            nc.vector.tensor_copy(w_spread[:, blocks, :, :],
+                                  w_turned[:, :, blocks].rearrange("p g b -> p b g").unsqueeze(3).to_broadcast([P, 16, 2, 16]))
+        for h in range(HALVES):
+            blocks = slice(16 * h, 16 * (h + 1))
+            nc.vector.transpose(weights[:, h * JH:(h + 1) * JH],
+                                w_spread[:, blocks, :, :].rearrange("p b g r -> p (b g r)"))
         load_plane(0, 1)
         load_plane(0, 2)
         load_plane(0, 3)
@@ -86,12 +103,12 @@ def tile_list_hway_kernel(tc, xT, wgt, wk_words, wk_scales, wv, bg, res, offs, o
         load_wv(1, 0)
         nc.sync.dma_start(wk_codes[:].bitcast(I32), wk_words.rearrange("a p b -> p a b").bitcast(I32))
         load_plane(1, 3)
-        load_res(0)
-        load_res(1)
-        load_res(2)
+        load_res(0, 0)
+        load_res(0, 1)
+        load_res(1, 0)
         load_wv(0, 1)
         load_wv(1, 1)
-        load_res(3)
+        load_res(1, 1)
 
         bias_turned = psum.tile([P, P], F32, name="ke")
         nc.tensor.transpose(bias_turned[:], bias_rows[:], identity[:])
@@ -164,42 +181,56 @@ def tile_list_hway_kernel(tc, xT, wgt, wk_words, wk_scales, wv, bg, res, offs, o
                         start=(a == 0 and u == 0 and b == 0),
                         stop=(a == PASSES - 1 and u == count - 1 and b + step == width))
 
-        def res_of(unit):
-            nt0, count, j0, width = unit
-            return res_sb[nt0 // 2][:, nt0 % 2:nt0 % 2 + count, j0:j0 + width]
+        gates = {}
+        diffs = {}
 
-        def finish(pair):
-            gates = []
-            diffs = []
-            for unit in pair:
+        def leave_banks(units):
+            nt0, count, j0, width = units[0]
+            block = (nt0 // 2, j0 // JH)
+            gate = work.tile([P, 2, JH], F32, name="gate")
+            diff = work.tile([P, 2, JH], F32, name="diff")
+            gates[block] = gate
+            diffs[block] = diff
+            for unit in units:
                 nt0, count, j0, width = unit
                 ke, ve = banks[unit]
-                gate = work.tile([P, count, width], F32, name="gate")
+                u0 = nt0 % 2
+                cols = slice(j0 % JH, j0 % JH + width)
                 for u in range(count):
-                    nc.scalar.activation(gate[:, u, :], ke[:, u, :], ACT.Sigmoid, bias=bias[:, nt0 + u:nt0 + u + 1])
-                diff = work.tile([P, count, width], F32, name="diff")
-                nc.vector.tensor_tensor(diff[:], ve[:], res_of(unit), ALU.subtract)
-                gates.append(gate)
-                diffs.append(diff)
-            for gate, diff in zip(gates, diffs):
-                nc.vector.tensor_tensor(diff[:], diff[:], gate[:], ALU.mult)
-            for unit, diff in zip(pair, diffs):
-                nt0, count, j0, width = unit
-                result = work.tile([P, count, width], F32, name="result")
-                rows = out[nt0 * P:(nt0 + count) * P, j0:j0 + width].rearrange("(u p) j -> p u j", p=P)
-                step = width // 2 if unit == later[-1] else width
-                for b in range(0, width, step):
-                    nc.vector.tensor_tensor(result[:, :, b:b + step], diff[:, :, b:b + step],
-                                            res_of(unit)[:, :, b:b + step], ALU.add)
-                    nc.sync.dma_start(rows[:, :, b:b + step], result[:, :, b:b + step])
+                    nc.scalar.activation(gate[:, u0 + u, cols], ke[:, u, :], ACT.Sigmoid,
+                                         bias=bias[:, nt0 + u:nt0 + u + 1])
+                nc.vector.tensor_tensor(diff[:, u0:u0 + count, cols], ve[:], res_sb[block][:, u0:u0 + count, cols],
+                                        ALU.subtract)
+
+        def part(tile, unit):
+            nt0, count, j0, width = unit
+            return tile[:, nt0 % 2:nt0 % 2 + count, j0 % JH:j0 % JH + width]
+
+        def block_key(unit):
+            return (unit[0] // 2, unit[2] // JH)
+
+        def apply_gate(units):
+            for unit in units:
+                block = block_key(unit)
+                nc.vector.tensor_tensor(part(diffs[block], unit), part(diffs[block], unit),
+                                        part(gates[block], unit), ALU.mult)
+
+        def add_res(pieces, shared):
+            block = block_key(pieces[0])
+            result = work.tile([P, 2, JH], F32, name="result")
+            for engine, piece in [(nc.gpsimd, p) for p in shared] + [(nc.vector, p) for p in pieces]:
+                engine.tensor_tensor(part(result, piece), part(diffs[block], piece), part(res_sb[block], piece), ALU.add)
+            return result
+
+        def store(result, pieces):
+            for piece in pieces:
+                nc.sync.dma_start(part(block_of(out, *block_key(piece)), piece), part(result, piece))
 
         JQ = JH // 2
         first = [(0, 2, 0, JQ), (0, 2, JQ, JQ), (0, 1, JH, JH), (1, 1, JH, JH)]
         later = [(2, 1, 0, JH), (3, 1, 0, JH), (2, 1, JH, JH), (3, 1, JH, JH)]
 
-        gather(0, 0, 0, JH)
-        gather(0, 0, JH, JH)
-        for i in range(1, PACK):
+        for i in range(PACK):
             gather(0, i, 0, J)
         gather(1, 0, 0, J)
         gather(1, 1, 0, J)
@@ -225,14 +256,28 @@ def tile_list_hway_kernel(tc, xT, wgt, wk_words, wk_scales, wv, bg, res, offs, o
         make_xq(1, JQ, JQ)
         multiply(first[1], 1)
         make_xq(1, JH, JQ)
-        finish(first[0:2])
+        leave_banks(first[0:2])
         make_xq(1, JH + JQ, JQ)
         multiply(first[2], 1)
         multiply(first[3], 1)
+        apply_gate(first[0:2])
+        leave_banks(first[2:4])
+        store(add_res([first[0], first[1]], []), [first[0], first[1]])
         make_vq(1)
-        finish(first[2:4])
-        for unit in later:
+        for unit in later[0:2]:
             multiply(unit, 0)
             multiply(unit, 1)
-        finish(later[0:2])
-        finish(later[2:4])
+        apply_gate(first[2:4])
+        leave_banks(later[0:2])
+        store(add_res([first[2], first[3]], []), [first[2], first[3]])
+        for unit in later[2:4]:
+            multiply(unit, 0)
+            multiply(unit, 1)
+        apply_gate(later[0:2])
+        leave_banks(later[2:4])
+        store(add_res([later[0], later[1]], []), [later[0], later[1]])
+        apply_gate(later[2:4])
+        result = work.tile([P, 2, JH], F32, name="result")
+        for piece in (later[2], (3, 1, JH, JQ), (3, 1, JH + JQ, JQ)):
+            nc.vector.tensor_tensor(part(result, piece), part(diffs[1, 1], piece), part(res_sb[1, 1], piece), ALU.add)
+            store(result, [piece])

@@ -4,7 +4,9 @@ import concourse.mybir as mybir
 from concourse.masks import make_identity
 
 K, N, T, J = 1024, 512, 2048, 1024
+HEADS = 8
 FLOPS = 2 * 2 * K * N * J
+BYTES = 4 * K * T + 4 * HEADS * J + K * N // 2 + K * N // 32 + 4 * K * N + 4 * N + 4 * N * J + 2 * HEADS * J + 4 * N * J
 
 F32 = mybir.dt.float32
 BF16 = mybir.dt.bfloat16
@@ -18,13 +20,22 @@ ALU = mybir.AluOpType
 ACT = mybir.ActivationFunctionType
 
 P = 128
+QUAD = 32
+GROUP = 16
 PACK = 4
 K_PASS = P * PACK
 PASSES = K // K_PASS
 JH = 512
-HALVES = J // JH
+JQ = 256
 NH = 256
 N_TILES = N // P
+
+UNITS = {
+    (0, 0): [(0, 2, 0, JQ), (0, 2, JQ, JQ)],
+    (0, 1): [(0, 1, JH, JH), (1, 1, JH, JH)],
+    (1, 0): [(2, 1, 0, JH), (3, 1, 0, JH)],
+    (1, 1): [(2, 1, JH, JH), (3, 1, JH, JH)],
+}
 
 
 def tile_list_hway_kernel(tc, xT, wgt, wk_words, wk_scales, wv, bg, res, offs, out):
@@ -34,26 +45,23 @@ def tile_list_hway_kernel(tc, xT, wgt, wk_words, wk_scales, wv, bg, res, offs, o
         work = ctx.enter_context(tc.tile_pool(name="work", bufs=3))
         psum = ctx.enter_context(tc.psum_pool(name="psum", bufs=4))
 
-        offsets = keep.tile([P, J // 16], U16, name="offsets")
+        offsets = keep.tile([P, J // GROUP], U16, name="offsets")
         weights = keep.tile([P, J], F32, name="weights", align_bytes=64)
         planes = [[keep.tile([P, T], F32, name="plane%d_%d" % (a, i), tag="plane%d_%d" % (a, i), align_bytes=64)
                    for i in range(PACK)] for a in range(PASSES)]
         wk_codes = keep.tile([P, PASSES, 2 * N], U8, name="wk_codes", align_bytes=64)
-        wk_plane = keep.tile([P, PASSES, N], U8, name="wk_plane", align_bytes=64)
+        wk_scale_rows = keep.tile([P, PASSES, N], U8, name="wk_scale_rows", align_bytes=64)
         bias = keep.tile([P, N_TILES], F32, name="bias")
         wv_raw = [[keep.tile([P, PACK, NH], F32, name="wv_raw%d_%d" % (a, m)) for m in range(2)] for a in range(PASSES)]
         wv_bf = [keep.tile([P, PASSES, NH, PACK], BF16, name="wv_bf%d" % m, align_bytes=64) for m in range(2)]
-        res_sb = {(m, h): keep.tile([P, 2, JH], F32, name="res%d_%d" % (m, h)) for m in range(2) for h in range(HALVES)}
-        warm = keep.tile([P, 8], F32, name="warm")
-        warm2 = keep.tile([P, 8], F32, name="warm2")
+        res_sb = {block: keep.tile([P, 2, JH], F32, name="res%d_%d" % block) for block in UNITS}
 
         bias_rows = keep.tile([P, P], F32, name="bias_rows")
         identity = keep.tile([P, P], F32, name="identity")
         make_identity(nc, identity[:])
         nc.vector.memset(bias_rows[:], 0.0)
-        nc.vector.memset(warm[:], 0.0)
-        nc.scalar.activation(warm2[:], warm[:], ACT.Sigmoid)
-        nc.vector.memset(wk_plane[:].rearrange("p a n -> p (a n)").bitcast(I32), 0)
+        nc.scalar.activation(bias_rows[:], bias_rows[:], ACT.Sigmoid)
+        nc.vector.memset(wk_scale_rows[:].rearrange("p a n -> p (a n)").bitcast(I32), 0)
 
         def load_plane(a, i):
             rows = xT[a * K_PASS:(a + 1) * K_PASS, :].rearrange("(p i) t -> p i t", i=PACK)
@@ -63,91 +71,97 @@ def tile_list_hway_kernel(tc, xT, wgt, wk_words, wk_scales, wv, bg, res, offs, o
             rows = wv[a * K_PASS:(a + 1) * K_PASS, :].rearrange("(p i) n -> p i n", i=PACK)
             nc.sync.dma_start(wv_raw[a][m][:], rows[:, :, m * NH:(m + 1) * NH])
 
-        def block_of(matrix, m, h):
+        def block_of(matrix, block):
+            m, h = block
             return matrix[m * NH:(m + 1) * NH, h * JH:(h + 1) * JH].rearrange("(u p) j -> p u j", p=P)
 
-        def load_res(m, h):
-            nc.sync.dma_start(res_sb[m, h][:], block_of(res, m, h))
+        def load_res(block):
+            nc.sync.dma_start(res_sb[block][:], block_of(res, block))
 
-        w_rows = keep.tile([P, 2, 32], F32, name="w_rows", align_bytes=64)
-        w_turned = keep.tile([P, 2, 32], F32, name="w_turned", align_bytes=64)
-        w_spread = keep.tile([P, 32, 2, 16], F32, name="w_spread", align_bytes=64)
-        for q in range(4):
-            nc.sync.dma_start(w_rows[32 * q:32 * q + 32, :, :],
-                            wgt[32 * q:32 * q + 32:16, :].rearrange("g (b s) -> b g s", s=32))
+        w_rows = keep.tile([P, 2, QUAD], F32, name="w_rows", align_bytes=64)
+        w_turned = keep.tile([P, 2, QUAD], F32, name="w_turned", align_bytes=64)
+        w_spread = keep.tile([P, J // QUAD, 2, GROUP], F32, name="w_spread", align_bytes=64)
+        for q in range(P // QUAD):
+            nc.sync.dma_start(w_rows[QUAD * q:QUAD * (q + 1), :, :],
+                              wgt[QUAD * q:QUAD * (q + 1):GROUP, :].rearrange("g (b s) -> b g s", s=QUAD))
         load_plane(0, 0)
         nc.sync.dma_start(offsets[:], offs)
         for g in range(2):
             nc.vector.transpose(w_turned[:, g, :], w_rows[:, g, :])
-        for h in range(HALVES):
-            blocks = slice(16 * h, 16 * (h + 1))
-            nc.vector.tensor_copy(w_spread[:, blocks, :, :],
-                                  w_turned[:, :, blocks].rearrange("p g b -> p b g").unsqueeze(3).to_broadcast([P, 16, 2, 16]))
-        for h in range(HALVES):
-            blocks = slice(16 * h, 16 * (h + 1))
+        half_blocks = JH // QUAD
+        for h, copy in enumerate((nc.vector.tensor_copy, nc.scalar.copy)):
+            b = slice(half_blocks * h, half_blocks * (h + 1))
+            copy(w_spread[:, b, :, :],
+                 w_turned[:, :, b].rearrange("p g b -> p b g").unsqueeze(3).to_broadcast([P, half_blocks, 2, GROUP]))
+        for h in range(2):
+            b = slice(half_blocks * h, half_blocks * (h + 1))
             nc.vector.transpose(weights[:, h * JH:(h + 1) * JH],
-                                w_spread[:, blocks, :, :].rearrange("p b g r -> p (b g r)"))
+                                w_spread[:, b, :, :].rearrange("p b g r -> p (b g r)"))
+
         load_plane(0, 1)
         load_plane(0, 2)
         load_plane(0, 3)
-        for q in range(4):
+        for q in range(P // QUAD):
             nc.sync.dma_start(
-                wk_plane[32 * q:32 * q + 4, :, :].bitcast(I32),
+                wk_scale_rows[QUAD * q:QUAD * q + 4, :, :].bitcast(I32),
                 wk_scales[:, 4 * q:4 * q + 4, :].rearrange("a r n -> r a n").bitcast(I32),
             )
         nc.sync.dma_start(bias_rows[0:N_TILES, :], bg.rearrange("(c p) -> c p", p=P))
         load_plane(1, 0)
         load_plane(1, 1)
         load_wv(0, 0)
-        load_plane(1, 2)
         load_wv(1, 0)
-        nc.sync.dma_start(wk_codes[:].bitcast(I32), wk_words.rearrange("a p b -> p a b").bitcast(I32))
+        load_plane(1, 2)
         load_plane(1, 3)
-        load_res(0, 0)
-        load_res(0, 1)
-        load_res(1, 0)
+        nc.sync.dma_start(wk_codes[:].bitcast(I32), wk_words.rearrange("a p b -> p a b").bitcast(I32))
+        load_res((0, 0))
+        load_res((0, 1))
+        load_res((1, 0))
         load_wv(0, 1)
         load_wv(1, 1)
-        load_res(1, 1)
+        load_res((1, 1))
 
         bias_turned = psum.tile([P, P], F32, name="ke")
         nc.tensor.transpose(bias_turned[:], bias_rows[:], identity[:])
         nc.scalar.copy(bias[:], bias_turned[:, 0:N_TILES])
 
-        def interleave(grouped, src):
-            nc.scalar.copy(
-                grouped.rearrange("p (c r) i -> p c i r", r=4),
-                src.rearrange("p i (c r) -> p c i r", r=4),
-            )
-
-        def operand(name, width, tag):
-            codes = keep.tile([P, width], U32, name=name + "_codes", tag=tag, align_bytes=64)
-            scales = keep.tile([P, width], U8, name=name + "_scales", align_bytes=64)
-            return codes, scales
-
         picked = [keep.tile([P, PACK, J], F32, name="picked%d" % a) for a in range(PASSES)]
+        xg_bf = {}
         xq = {}
         vq = {}
+
+        def mx_operand(name, width, tag):
+            codes = keep.tile([P, width], U32, name=name + "_codes", tag=tag, align_bytes=64)
+            scales = keep.tile([P, width], U8, name=name + "_scales", align_bytes=64)
+            return codes[:], scales[:]
 
         def gather(a, i, j0, width):
             nc.vector.tensor_tensor(
                 picked[a][:, i, j0:j0 + width],
-                planes[a][i][:].indirect(offsets[:, j0 // 16:(j0 + width) // 16]),
+                planes[a][i][:].indirect(offsets[:, j0 // GROUP:(j0 + width) // GROUP]),
                 weights[:, j0:j0 + width],
                 ALU.mult,
             )
 
-        def make_xq(a, j0, width):
-            grouped = keep.tile([P, width, PACK], BF16, name="xg_bf%d_%d" % (a, j0), align_bytes=64)
-            interleave(grouped[:], picked[a][:, :, j0:j0 + width])
+        def lay_pair(a, pair, j0, width):
+            i = slice(2 * pair, 2 * pair + 2)
+            nc.scalar.copy(xg_bf[a, j0][:, :, i], picked[a][:, i, j0:j0 + width].rearrange("p i w -> p w i"))
+
+        def begin_xq(a, j0, width):
+            xg_bf[a, j0] = keep.tile([P, width, PACK], BF16, name="xg_bf%d_%d" % (a, j0), align_bytes=64)
+            lay_pair(a, 0, j0, width)
+
+        def finish_xq(a, j0, width):
+            lay_pair(a, 1, j0, width)
             codes, scales = xq[a, j0 // JH]
-            c0 = j0 % JH
-            nc.vector.quantize_mx(codes[:, c0:c0 + width].bitcast(FP8X4), scales[:, c0:c0 + width],
-                                  grouped[:].rearrange("p w i -> p (w i)"))
+            cols = slice(j0 % JH, j0 % JH + width)
+            nc.vector.quantize_mx(codes[:, cols].bitcast(FP8X4), scales[:, cols],
+                                  xg_bf[a, j0][:].rearrange("p w i -> p (w i)"))
 
         def make_vq(m):
             for a in range(PASSES):
-                interleave(wv_bf[m][:, a, :, :], wv_raw[a][m][:])
+                nc.scalar.copy(wv_bf[m][:, a, :, :].rearrange("p (c r) i -> p c i r", r=4),
+                               wv_raw[a][m][:].rearrange("p i (c r) -> p c i r", r=4))
             codes, scales = vq[m]
             nc.vector.quantize_mx(codes.bitcast(FP8X4), scales, wv_bf[m][:].rearrange("p a w i -> p (a w i)"))
 
@@ -160,124 +174,103 @@ def tile_list_hway_kernel(tc, xT, wgt, wk_words, wk_scales, wv, bg, res, offs, o
                 ve = psum.tile([P, count, width], F32, name="ve")
                 banks[unit] = (ke, ve)
             ke, ve = banks[unit]
+            x_codes, x_scales = xq[a, j0 // JH]
             c0 = j0 % JH
-            codes, scales = xq[a, j0 // JH]
             for u in range(count):
                 nt = nt0 + u
                 v_codes, v_scales = vq[nt // 2]
                 v0 = a * NH + (nt % 2) * P
                 nc.tensor.matmul_mx(
                     ve[:, u, :], lhsT=v_codes[:, v0:v0 + P].bitcast(FP8X4), lhsT_scale=v_scales[:, v0:v0 + P],
-                    rhs=codes[:, c0:c0 + width].bitcast(FP8X4), rhs_scale=scales[:, c0:c0 + width],
+                    rhs=x_codes[:, c0:c0 + width].bitcast(FP8X4), rhs_scale=x_scales[:, c0:c0 + width],
                     start=(a == 0 and u == 0), stop=(a == PASSES - 1 and u == count - 1))
-            step = width if width == JH else P
+            step = JH if width == JH else P
             for u in range(count):
                 nt = nt0 + u
                 for b in range(0, width, step):
                     nc.tensor.matmul_mx(
                         ke[:, u, b:b + step], lhsT=wk_codes[:, a, 2 * P * nt:2 * P * (nt + 1)].bitcast(FP4X4),
-                        lhsT_scale=wk_plane[:, a, P * nt:P * (nt + 1)],
-                        rhs=codes[:, c0 + b:c0 + b + step].bitcast(FP8X4), rhs_scale=scales[:, c0 + b:c0 + b + step],
+                        lhsT_scale=wk_scale_rows[:, a, P * nt:P * (nt + 1)],
+                        rhs=x_codes[:, c0 + b:c0 + b + step].bitcast(FP8X4),
+                        rhs_scale=x_scales[:, c0 + b:c0 + b + step],
                         start=(a == 0 and u == 0 and b == 0),
                         stop=(a == PASSES - 1 and u == count - 1 and b + step == width))
-
-        gates = {}
-        diffs = {}
-
-        def leave_banks(units):
-            nt0, count, j0, width = units[0]
-            block = (nt0 // 2, j0 // JH)
-            gate = work.tile([P, 2, JH], F32, name="gate")
-            diff = work.tile([P, 2, JH], F32, name="diff")
-            gates[block] = gate
-            diffs[block] = diff
-            for unit in units:
-                nt0, count, j0, width = unit
-                ke, ve = banks[unit]
-                u0 = nt0 % 2
-                cols = slice(j0 % JH, j0 % JH + width)
-                for u in range(count):
-                    nc.scalar.activation(gate[:, u0 + u, cols], ke[:, u, :], ACT.Sigmoid,
-                                         bias=bias[:, nt0 + u:nt0 + u + 1])
-                nc.vector.tensor_tensor(diff[:, u0:u0 + count, cols], ve[:], res_sb[block][:, u0:u0 + count, cols],
-                                        ALU.subtract)
 
         def part(tile, unit):
             nt0, count, j0, width = unit
             return tile[:, nt0 % 2:nt0 % 2 + count, j0 % JH:j0 % JH + width]
 
-        def block_key(unit):
-            return (unit[0] // 2, unit[2] // JH)
+        gates = {}
+        diffs = {}
 
-        def apply_gate(units):
-            for unit in units:
-                block = block_key(unit)
+        def leave_banks(block):
+            gates[block] = work.tile([P, 2, JH], F32, name="gate")
+            diffs[block] = work.tile([P, 2, JH], F32, name="diff")
+            for unit in UNITS[block]:
+                nt0, count = unit[0:2]
+                ke, ve = banks[unit]
+                for u in range(count):
+                    nc.scalar.activation(part(gates[block], unit)[:, u, :], ke[:, u, :], ACT.Sigmoid,
+                                         bias=bias[:, nt0 + u:nt0 + u + 1])
+                nc.vector.tensor_tensor(part(diffs[block], unit), ve[:], part(res_sb[block], unit), ALU.subtract)
+
+        def apply_gate(block):
+            for unit in UNITS[block]:
                 nc.vector.tensor_tensor(part(diffs[block], unit), part(diffs[block], unit),
                                         part(gates[block], unit), ALU.mult)
 
-        def add_res(pieces, shared):
-            block = block_key(pieces[0])
+        def sum_and_store(block, pieces):
             result = work.tile([P, 2, JH], F32, name="result")
-            for engine, piece in [(nc.gpsimd, p) for p in shared] + [(nc.vector, p) for p in pieces]:
-                engine.tensor_tensor(part(result, piece), part(diffs[block], piece), part(res_sb[block], piece), ALU.add)
-            return result
-
-        def store(result, pieces):
             for piece in pieces:
-                nc.sync.dma_start(part(block_of(out, *block_key(piece)), piece), part(result, piece))
+                nc.vector.tensor_tensor(part(result, piece), part(diffs[block], piece), part(res_sb[block], piece),
+                                        ALU.add)
+                nc.sync.dma_start(part(block_of(out, block), piece), part(result, piece))
 
-        JQ = JH // 2
-        first = [(0, 2, 0, JQ), (0, 2, JQ, JQ), (0, 1, JH, JH), (1, 1, JH, JH)]
-        later = [(2, 1, 0, JH), (3, 1, 0, JH), (2, 1, JH, JH), (3, 1, JH, JH)]
-
-        for i in range(PACK):
-            gather(0, i, 0, J)
+        gather(0, 0, 0, J)
+        gather(0, 1, 0, J)
+        for h in range(2):
+            begin_xq(0, h * JH, JH)
+        gather(0, 2, 0, J)
+        gather(0, 3, 0, J)
         gather(1, 0, 0, J)
         gather(1, 1, 0, J)
-        xq[0, 0] = operand("xg0_0", JH, "plane1_1")
-        make_xq(0, 0, JH)
+        codes, scales = mx_operand("xg0", J, "plane1_1")
+        for h in range(2):
+            xq[0, h] = (codes[:, h * JH:(h + 1) * JH], scales[:, h * JH:(h + 1) * JH])
+            finish_xq(0, h * JH, JH)
         gather(1, 2, 0, J)
-        both = operand("behind6", 2 * JH, "plane1_2")
-        vq[0] = (both[0][:, 0:JH], both[1][:, 0:JH])
-        xq[0, 1] = (both[0][:, JH:J], both[1][:, JH:J])
+        vq[0] = mx_operand("wv0", PASSES * NH, "plane1_2")
         make_vq(0)
-        make_xq(0, JH, JH)
-        for unit in first:
+        for j0 in range(0, J, JQ):
+            begin_xq(1, j0, JQ)
+        for unit in UNITS[0, 0] + UNITS[0, 1]:
             multiply(unit, 0)
-        for h in range(HALVES):
-            xq[1, h] = operand("xg1_%d" % h, JH, "xg1_%d" % h)
-        later_v = operand("wv1", JH, "wv1")
-        vq[1] = (later_v[0][:], later_v[1][:])
+        for h in range(2):
+            xq[1, h] = mx_operand("xg1_%d" % h, JH, "xg1_%d" % h)
+        vq[1] = mx_operand("wv1", PASSES * NH, "wv1")
+
         gather(1, PACK - 1, 0, JQ)
         gather(1, PACK - 1, JQ, JQ)
         gather(1, PACK - 1, JH, JH)
-        make_xq(1, 0, JQ)
-        multiply(first[0], 1)
-        make_xq(1, JQ, JQ)
-        multiply(first[1], 1)
-        make_xq(1, JH, JQ)
-        leave_banks(first[0:2])
-        make_xq(1, JH + JQ, JQ)
-        multiply(first[2], 1)
-        multiply(first[3], 1)
-        apply_gate(first[0:2])
-        leave_banks(first[2:4])
-        store(add_res([first[0], first[1]], []), [first[0], first[1]])
+        for unit in UNITS[0, 0]:
+            finish_xq(1, unit[2], JQ)
+            multiply(unit, 1)
+        finish_xq(1, JH, JQ)
+        leave_banks((0, 0))
+        finish_xq(1, JH + JQ, JQ)
+        for unit in UNITS[0, 1]:
+            multiply(unit, 1)
+
+        apply_gate((0, 0))
+        leave_banks((0, 1))
+        sum_and_store((0, 0), UNITS[0, 0])
         make_vq(1)
-        for unit in later[0:2]:
-            multiply(unit, 0)
-            multiply(unit, 1)
-        apply_gate(first[2:4])
-        leave_banks(later[0:2])
-        store(add_res([first[2], first[3]], []), [first[2], first[3]])
-        for unit in later[2:4]:
-            multiply(unit, 0)
-            multiply(unit, 1)
-        apply_gate(later[0:2])
-        leave_banks(later[2:4])
-        store(add_res([later[0], later[1]], []), [later[0], later[1]])
-        apply_gate(later[2:4])
-        result = work.tile([P, 2, JH], F32, name="result")
-        for piece in (later[2], (3, 1, JH, JQ), (3, 1, JH + JQ, JQ)):
-            nc.vector.tensor_tensor(part(result, piece), part(diffs[1, 1], piece), part(res_sb[1, 1], piece), ALU.add)
-            store(result, [piece])
+        for done, following in (((0, 1), (1, 0)), ((1, 0), (1, 1))):
+            for unit in UNITS[following]:
+                for a in range(PASSES):
+                    multiply(unit, a)
+            apply_gate(done)
+            leave_banks(following)
+            sum_and_store(done, UNITS[done])
+        apply_gate((1, 1))
+        sum_and_store((1, 1), [UNITS[1, 1][0], (3, 1, JH, JQ), (3, 1, JH + JQ, JQ)])

@@ -49,7 +49,7 @@ def tile_list_hway_kernel(tc, xT, wgt, wk_words, wk_scales, wv, bg, res, offs, o
         weights = keep.tile([P, J], F32, name="weights", align_bytes=64)
         planes = [[keep.tile([P, T], F32, name="plane%d_%d" % (a, i), tag="plane%d_%d" % (a, i), align_bytes=64)
                    for i in range(PACK)] for a in range(PASSES)]
-        wk_codes = keep.tile([P, PASSES, 2 * N], U8, name="wk_codes", align_bytes=64)
+        wk_codes = [keep.tile([P, 2 * N], U8, name="wk_codes%d" % a, align_bytes=64) for a in range(PASSES)]
         wk_scale_rows = keep.tile([P, PASSES, N], U8, name="wk_scale_rows", align_bytes=64)
         bias = keep.tile([P, N_TILES], F32, name="bias")
         wv_raw = [[keep.tile([P, PACK, NH], F32, name="wv_raw%d_%d" % (a, m)) for m in range(2)] for a in range(PASSES)]
@@ -71,6 +71,9 @@ def tile_list_hway_kernel(tc, xT, wgt, wk_words, wk_scales, wv, bg, res, offs, o
             rows = wv[a * K_PASS:(a + 1) * K_PASS, :].rearrange("(p i) n -> p i n", i=PACK)
             nc.sync.dma_start(wv_raw[a][m][:], rows[:, :, m * NH:(m + 1) * NH])
 
+        def load_wk(a):
+            nc.sync.dma_start(wk_codes[a][:].bitcast(I32), wk_words[a].bitcast(I32))
+
         def block_of(matrix, block):
             m, h = block
             return matrix[m * NH:(m + 1) * NH, h * JH:(h + 1) * JH].rearrange("(u p) j -> p u j", p=P)
@@ -89,10 +92,11 @@ def tile_list_hway_kernel(tc, xT, wgt, wk_words, wk_scales, wv, bg, res, offs, o
         for g in range(2):
             nc.vector.transpose(w_turned[:, g, :], w_rows[:, g, :])
         half_blocks = JH // QUAD
-        for h, copy in enumerate((nc.vector.tensor_copy, nc.scalar.copy)):
+        for h in range(2):
             b = slice(half_blocks * h, half_blocks * (h + 1))
-            copy(w_spread[:, b, :, :],
-                 w_turned[:, :, b].rearrange("p g b -> p b g").unsqueeze(3).to_broadcast([P, half_blocks, 2, GROUP]))
+            nc.vector.tensor_copy(
+                w_spread[:, b, :, :],
+                w_turned[:, :, b].rearrange("p g b -> p b g").unsqueeze(3).to_broadcast([P, half_blocks, 2, GROUP]))
         for h in range(2):
             b = slice(half_blocks * h, half_blocks * (h + 1))
             nc.vector.transpose(weights[:, h * JH:(h + 1) * JH],
@@ -110,10 +114,11 @@ def tile_list_hway_kernel(tc, xT, wgt, wk_words, wk_scales, wv, bg, res, offs, o
         load_plane(1, 0)
         load_plane(1, 1)
         load_wv(0, 0)
-        load_wv(1, 0)
         load_plane(1, 2)
+        load_wv(1, 0)
+        load_wk(0)
         load_plane(1, 3)
-        nc.sync.dma_start(wk_codes[:].bitcast(I32), wk_words.rearrange("a p b -> p a b").bitcast(I32))
+        load_wk(1)
         load_res((0, 0))
         load_res((0, 1))
         load_res((1, 0))
@@ -126,7 +131,6 @@ def tile_list_hway_kernel(tc, xT, wgt, wk_words, wk_scales, wv, bg, res, offs, o
         nc.scalar.copy(bias[:], bias_turned[:, 0:N_TILES])
 
         picked = [keep.tile([P, PACK, J], F32, name="picked%d" % a) for a in range(PASSES)]
-        xg_bf = {}
         xq = {}
         vq = {}
 
@@ -143,25 +147,20 @@ def tile_list_hway_kernel(tc, xT, wgt, wk_words, wk_scales, wv, bg, res, offs, o
                 ALU.mult,
             )
 
-        def lay_pair(a, pair, j0, width):
-            i = slice(2 * pair, 2 * pair + 2)
-            nc.scalar.copy(xg_bf[a, j0][:, :, i], picked[a][:, i, j0:j0 + width].rearrange("p i w -> p w i"))
+        def interleave(grouped, rows):
+            nc.scalar.copy(grouped.rearrange("p (c r) i -> p c i r", r=4), rows.rearrange("p i (c r) -> p c i r", r=4))
 
-        def begin_xq(a, j0, width):
-            xg_bf[a, j0] = keep.tile([P, width, PACK], BF16, name="xg_bf%d_%d" % (a, j0), align_bytes=64)
-            lay_pair(a, 0, j0, width)
-
-        def finish_xq(a, j0, width):
-            lay_pair(a, 1, j0, width)
+        def make_xq(a, j0, width):
+            grouped = keep.tile([P, width, PACK], BF16, name="xg_bf%d_%d" % (a, j0), align_bytes=64)
+            interleave(grouped[:], picked[a][:, :, j0:j0 + width])
             codes, scales = xq[a, j0 // JH]
             cols = slice(j0 % JH, j0 % JH + width)
             nc.vector.quantize_mx(codes[:, cols].bitcast(FP8X4), scales[:, cols],
-                                  xg_bf[a, j0][:].rearrange("p w i -> p (w i)"))
+                                  grouped[:].rearrange("p w i -> p (w i)"))
 
         def make_vq(m):
             for a in range(PASSES):
-                nc.scalar.copy(wv_bf[m][:, a, :, :].rearrange("p (c r) i -> p c i r", r=4),
-                               wv_raw[a][m][:].rearrange("p i (c r) -> p c i r", r=4))
+                interleave(wv_bf[m][:, a, :, :], wv_raw[a][m][:])
             codes, scales = vq[m]
             nc.vector.quantize_mx(codes.bitcast(FP8X4), scales, wv_bf[m][:].rearrange("p a w i -> p (a w i)"))
 
@@ -189,7 +188,7 @@ def tile_list_hway_kernel(tc, xT, wgt, wk_words, wk_scales, wv, bg, res, offs, o
                 nt = nt0 + u
                 for b in range(0, width, step):
                     nc.tensor.matmul_mx(
-                        ke[:, u, b:b + step], lhsT=wk_codes[:, a, 2 * P * nt:2 * P * (nt + 1)].bitcast(FP4X4),
+                        ke[:, u, b:b + step], lhsT=wk_codes[a][:, 2 * P * nt:2 * P * (nt + 1)].bitcast(FP4X4),
                         lhsT_scale=wk_scale_rows[:, a, P * nt:P * (nt + 1)],
                         rhs=x_codes[:, c0 + b:c0 + b + step].bitcast(FP8X4),
                         rhs_scale=x_scales[:, c0 + b:c0 + b + step],
@@ -226,23 +225,18 @@ def tile_list_hway_kernel(tc, xT, wgt, wk_words, wk_scales, wv, bg, res, offs, o
                                         ALU.add)
                 nc.sync.dma_start(part(block_of(out, block), piece), part(result, piece))
 
-        gather(0, 0, 0, J)
-        gather(0, 1, 0, J)
-        for h in range(2):
-            begin_xq(0, h * JH, JH)
-        gather(0, 2, 0, J)
-        gather(0, 3, 0, J)
+        for i in range(PACK):
+            gather(0, i, 0, J)
         gather(1, 0, 0, J)
         gather(1, 1, 0, J)
-        codes, scales = mx_operand("xg0", J, "plane1_1")
-        for h in range(2):
-            xq[0, h] = (codes[:, h * JH:(h + 1) * JH], scales[:, h * JH:(h + 1) * JH])
-            finish_xq(0, h * JH, JH)
+        xq[0, 0] = mx_operand("xg0_0", JH, "plane1_1")
+        make_xq(0, 0, JH)
         gather(1, 2, 0, J)
-        vq[0] = mx_operand("wv0", PASSES * NH, "plane1_2")
+        codes, scales = mx_operand("wv0_xg0_1", PASSES * NH + JH, "plane1_2")
+        vq[0] = (codes[:, :PASSES * NH], scales[:, :PASSES * NH])
+        xq[0, 1] = (codes[:, PASSES * NH:], scales[:, PASSES * NH:])
         make_vq(0)
-        for j0 in range(0, J, JQ):
-            begin_xq(1, j0, JQ)
+        make_xq(0, JH, JH)
         for unit in UNITS[0, 0] + UNITS[0, 1]:
             multiply(unit, 0)
         for h in range(2):
@@ -253,11 +247,11 @@ def tile_list_hway_kernel(tc, xT, wgt, wk_words, wk_scales, wv, bg, res, offs, o
         gather(1, PACK - 1, JQ, JQ)
         gather(1, PACK - 1, JH, JH)
         for unit in UNITS[0, 0]:
-            finish_xq(1, unit[2], JQ)
+            make_xq(1, unit[2], JQ)
             multiply(unit, 1)
-        finish_xq(1, JH, JQ)
+        make_xq(1, JH, JQ)
         leave_banks((0, 0))
-        finish_xq(1, JH + JQ, JQ)
+        make_xq(1, JH + JQ, JQ)
         for unit in UNITS[0, 1]:
             multiply(unit, 1)
 

@@ -30,19 +30,15 @@ JQ = 256
 NH = 256
 N_TILES = N // P
 
-UNITS = {
-    (0, 0): [(0, 2, 0, JQ), (0, 2, JQ, JQ)],
-    (0, 1): [(0, 1, JH, JH), (1, 1, JH, JH)],
-    (1, 0): [(2, 1, 0, JH), (3, 1, 0, JH)],
-    (1, 1): [(2, 1, JH, JH), (3, 1, JH, JH)],
-}
+UNITS = [(0, 2, 0, JQ), (0, 2, JQ, JQ), (0, 2, JH, JQ), (0, 2, JH + JQ, JQ),
+         (2, 1, 0, JH), (2, 1, JH, JH), (3, 1, 0, JH), (3, 1, JH, JH)]
 
 
 def tile_list_hway_kernel(tc, xT, wgt, wk_words, wk_scales, wv, bg, res, offs, out):
     nc = tc.nc
     with ExitStack() as ctx:
         keep = ctx.enter_context(tc.tile_pool(name="keep", bufs=1))
-        work = ctx.enter_context(tc.tile_pool(name="work", bufs=3))
+        work = ctx.enter_context(tc.tile_pool(name="work", bufs=4))
         psum = ctx.enter_context(tc.psum_pool(name="psum", bufs=4))
 
         offsets = keep.tile([P, J // GROUP], U16, name="offsets")
@@ -53,8 +49,7 @@ def tile_list_hway_kernel(tc, xT, wgt, wk_words, wk_scales, wv, bg, res, offs, o
         wk_scale_rows = keep.tile([P, PASSES, N], U8, name="wk_scale_rows", align_bytes=64)
         bias = keep.tile([P, N_TILES], F32, name="bias")
         wv_raw = [[keep.tile([P, PACK, NH], F32, name="wv_raw%d_%d" % (a, m)) for m in range(2)] for a in range(PASSES)]
-        wv_bf = [keep.tile([P, PASSES, NH, PACK], BF16, name="wv_bf%d" % m, align_bytes=64) for m in range(2)]
-        res_sb = {block: keep.tile([P, 2, JH], F32, name="res%d_%d" % block) for block in UNITS}
+        res_sb = [keep.tile([P, unit[1], unit[3]], F32, name="res%d" % u, tag="res%d" % u, align_bytes=64) for u, unit in enumerate(UNITS)]
 
         bias_rows = keep.tile([P, P], F32, name="bias_rows")
         identity = keep.tile([P, P], F32, name="identity")
@@ -74,12 +69,12 @@ def tile_list_hway_kernel(tc, xT, wgt, wk_words, wk_scales, wv, bg, res, offs, o
         def load_wk(a):
             nc.sync.dma_start(wk_codes[a][:].bitcast(I32), wk_words[a].bitcast(I32))
 
-        def block_of(matrix, block):
-            m, h = block
-            return matrix[m * NH:(m + 1) * NH, h * JH:(h + 1) * JH].rearrange("(u p) j -> p u j", p=P)
+        def unit_of(matrix, u):
+            nt0, count, j0, width = UNITS[u]
+            return matrix[nt0 * P:(nt0 + count) * P, j0:j0 + width].rearrange("(c p) j -> p c j", p=P)
 
-        def load_res(block):
-            nc.sync.dma_start(res_sb[block][:], block_of(res, block))
+        def load_res(u):
+            nc.sync.dma_start(res_sb[u][:], unit_of(res, u))
 
         w_rows = keep.tile([P, 2, QUAD], F32, name="w_rows", align_bytes=64)
         w_turned = keep.tile([P, 2, QUAD], F32, name="w_turned", align_bytes=64)
@@ -119,16 +114,16 @@ def tile_list_hway_kernel(tc, xT, wgt, wk_words, wk_scales, wv, bg, res, offs, o
         load_wk(0)
         load_plane(1, 3)
         load_wk(1)
-        load_res((0, 0))
-        load_res((0, 1))
-        load_res((1, 0))
+        for u in range(4):
+            load_res(u)
         load_wv(0, 1)
         load_wv(1, 1)
-        load_res((1, 1))
+        for u in range(4, 8):
+            load_res(u)
 
-        bias_turned = psum.tile([P, P], F32, name="ke")
+        bias_turned = psum.tile([P, P], F32, name="ke", bufs=3)
         nc.tensor.transpose(bias_turned[:], bias_rows[:], identity[:])
-        nc.scalar.copy(bias[:], bias_turned[:, 0:N_TILES])
+        nc.scalar.mul(bias[:], bias_turned[:, 0:N_TILES], -1.0)
 
         picked = [keep.tile([P, PACK, J], F32, name="picked%d" % a) for a in range(PASSES)]
         xq = {}
@@ -150,39 +145,37 @@ def tile_list_hway_kernel(tc, xT, wgt, wk_words, wk_scales, wv, bg, res, offs, o
         def interleave(grouped, rows):
             nc.scalar.copy(grouped.rearrange("p (c r) i -> p c i r", r=4), rows.rearrange("p i (c r) -> p c i r", r=4))
 
-        def make_xq(a, j0, width):
-            grouped = keep.tile([P, width, PACK], BF16, name="xg_bf%d_%d" % (a, j0), align_bytes=64)
+        def make_xq(a, j0, width, tag):
+            grouped = keep.tile([P, width, PACK], BF16, name="xg_bf%d_%d" % (a, j0), tag=tag, align_bytes=64)
             interleave(grouped[:], picked[a][:, :, j0:j0 + width])
             codes, scales = xq[a, j0 // JH]
             cols = slice(j0 % JH, j0 % JH + width)
             nc.vector.quantize_mx(codes[:, cols].bitcast(FP8X4), scales[:, cols],
                                   grouped[:].rearrange("p w i -> p (w i)"))
 
-        def make_vq(m):
+        def make_vq(nt0, count, tag):
+            width = count * P
+            grouped = keep.tile([P, PASSES, width, PACK], BF16, name="wv_bf%d" % nt0, align_bytes=64)
+            c0 = (nt0 % 2) * P
             for a in range(PASSES):
-                interleave(wv_bf[m][:, a, :, :], wv_raw[a][m][:])
-            codes, scales = vq[m]
-            nc.vector.quantize_mx(codes.bitcast(FP8X4), scales, wv_bf[m][:].rearrange("p a w i -> p (a w i)"))
+                interleave(grouped[:, a, :, :], wv_raw[a][nt0 // 2][:, :, c0:c0 + width])
+            codes, scales = mx_operand("wv%d" % nt0, PASSES * width, tag)
+            nc.vector.quantize_mx(codes.bitcast(FP8X4), scales, grouped[:].rearrange("p a w i -> p (a w i)"))
+            for c in range(count):
+                for a in range(PASSES):
+                    cols = slice(a * width + c * P, a * width + (c + 1) * P)
+                    vq[a, nt0 + c] = (codes[:, cols], scales[:, cols])
 
-        banks = {}
+        ke_banks = {}
+        ve_banks = {}
 
-        def multiply(unit, a):
-            nt0, count, j0, width = unit
+        def gate_sum(index, a):
+            nt0, count, j0, width = UNITS[index]
             if a == 0:
-                ke = psum.tile([P, count, width], F32, name="ke")
-                ve = psum.tile([P, count, width], F32, name="ve")
-                banks[unit] = (ke, ve)
-            ke, ve = banks[unit]
+                ke_banks[index] = psum.tile([P, count, width], F32, name="ke", bufs=3)
+            ke = ke_banks[index]
             x_codes, x_scales = xq[a, j0 // JH]
             c0 = j0 % JH
-            for u in range(count):
-                nt = nt0 + u
-                v_codes, v_scales = vq[nt // 2]
-                v0 = a * NH + (nt % 2) * P
-                nc.tensor.matmul_mx(
-                    ve[:, u, :], lhsT=v_codes[:, v0:v0 + P].bitcast(FP8X4), lhsT_scale=v_scales[:, v0:v0 + P],
-                    rhs=x_codes[:, c0:c0 + width].bitcast(FP8X4), rhs_scale=x_scales[:, c0:c0 + width],
-                    start=(a == 0 and u == 0), stop=(a == PASSES - 1 and u == count - 1))
             step = JH if width == JH else P
             for u in range(count):
                 nt = nt0 + u
@@ -195,76 +188,89 @@ def tile_list_hway_kernel(tc, xT, wgt, wk_words, wk_scales, wv, bg, res, offs, o
                         start=(a == 0 and u == 0 and b == 0),
                         stop=(a == PASSES - 1 and u == count - 1 and b + step == width))
 
-        def part(tile, unit):
-            nt0, count, j0, width = unit
-            return tile[:, nt0 % 2:nt0 % 2 + count, j0 % JH:j0 % JH + width]
+        def value_sum(index, a):
+            nt0, count, j0, width = UNITS[index]
+            if a == 0:
+                ve_banks[index] = psum.tile([P, count, width], F32, name="ve", bufs=5)
+            ve = ve_banks[index]
+            x_codes, x_scales = xq[a, j0 // JH]
+            c0 = j0 % JH
+            for u in range(count):
+                v_codes, v_scales = vq[a, nt0 + u]
+                nc.tensor.matmul_mx(
+                    ve[:, u, :], lhsT=v_codes.bitcast(FP8X4), lhsT_scale=v_scales,
+                    rhs=x_codes[:, c0:c0 + width].bitcast(FP8X4), rhs_scale=x_scales[:, c0:c0 + width],
+                    start=(a == 0 and u == 0), stop=(a == PASSES - 1 and u == count - 1))
 
-        gates = {}
+        def multiply(index, a):
+            gate_sum(index, a)
+            value_sum(index, a)
+
         diffs = {}
 
-        def leave_banks(block):
-            gates[block] = work.tile([P, 2, JH], F32, name="gate")
-            diffs[block] = work.tile([P, 2, JH], F32, name="diff")
-            for unit in UNITS[block]:
-                nt0, count = unit[0:2]
-                ke, ve = banks[unit]
-                for u in range(count):
-                    nc.scalar.activation(part(gates[block], unit)[:, u, :], ke[:, u, :], ACT.Sigmoid,
-                                         bias=bias[:, nt0 + u:nt0 + u + 1])
-                nc.vector.tensor_tensor(part(diffs[block], unit), ve[:], part(res_sb[block], unit), ALU.subtract)
+        def open_unit(index, engine):
+            nt0, count, j0, width = UNITS[index]
+            ke, ve = ke_banks[index], ve_banks[index]
+            rest = work.tile([P, count, width], F32, name="rest")
+            diff = work.tile([P, count, width], F32, name="diff", bufs=4)
+            diffs[index] = diff
+            for c in range(count):
+                nc.scalar.activation(rest[:, c, :], ke[:, c, :], ACT.Sigmoid,
+                                     bias=bias[:, nt0 + c:nt0 + c + 1], scale=-1.0)
+            nc.vector.tensor_tensor(diff[:], ve[:], res_sb[index][:], ALU.subtract)
+            engine.tensor_tensor(diff[:], diff[:], rest[:], ALU.mult)
 
-        def apply_gate(block):
-            for unit in UNITS[block]:
-                nc.vector.tensor_tensor(part(diffs[block], unit), part(diffs[block], unit),
-                                        part(gates[block], unit), ALU.mult)
-
-        def sum_and_store(block, pieces):
-            result = work.tile([P, 2, JH], F32, name="result")
-            for piece in pieces:
-                nc.vector.tensor_tensor(part(result, piece), part(diffs[block], piece), part(res_sb[block], piece),
-                                        ALU.add)
-                nc.sync.dma_start(part(block_of(out, block), piece), part(result, piece))
+        def close_unit(index, pieces):
+            nt0, count, j0, width = UNITS[index]
+            result = keep.tile([P, count, width], F32, name="result%d" % index, tag="res%d" % (index + 1), align_bytes=64)
+            step = width // pieces
+            for c0 in range(0, width, step):
+                cols = slice(c0, c0 + step)
+                nc.vector.tensor_tensor(result[:, :, cols], ve_banks[index][:, :, cols], diffs[index][:, :, cols],
+                                        ALU.subtract)
+                nc.sync.dma_start(unit_of(out, index)[:, :, cols], result[:, :, cols])
 
         for i in range(PACK):
             gather(0, i, 0, J)
         gather(1, 0, 0, J)
         gather(1, 1, 0, J)
         xq[0, 0] = mx_operand("xg0_0", JH, "plane1_1")
-        make_xq(0, 0, JH)
+        make_xq(0, 0, JH, "bf00")
         gather(1, 2, 0, J)
-        codes, scales = mx_operand("wv0_xg0_1", PASSES * NH + JH, "plane1_2")
-        vq[0] = (codes[:, :PASSES * NH], scales[:, :PASSES * NH])
-        xq[0, 1] = (codes[:, PASSES * NH:], scales[:, PASSES * NH:])
-        make_vq(0)
-        make_xq(0, JH, JH)
-        for unit in UNITS[0, 0] + UNITS[0, 1]:
-            multiply(unit, 0)
+        make_vq(0, 2, "plane1_2")
+        multiply(0, 0)
+        multiply(1, 0)
         for h in range(2):
             xq[1, h] = mx_operand("xg1_%d" % h, JH, "xg1_%d" % h)
-        vq[1] = mx_operand("wv1", PASSES * NH, "wv1")
 
         gather(1, PACK - 1, 0, JQ)
         gather(1, PACK - 1, JQ, JQ)
         gather(1, PACK - 1, JH, JH)
-        for unit in UNITS[0, 0]:
-            make_xq(1, unit[2], JQ)
-            multiply(unit, 1)
-        make_xq(1, JH, JQ)
-        leave_banks((0, 0))
-        make_xq(1, JH + JQ, JQ)
-        for unit in UNITS[0, 1]:
-            multiply(unit, 1)
-
-        apply_gate((0, 0))
-        leave_banks((0, 1))
-        sum_and_store((0, 0), UNITS[0, 0])
-        make_vq(1)
-        for done, following in (((0, 1), (1, 0)), ((1, 0), (1, 1))):
-            for unit in UNITS[following]:
+        xq[0, 1] = mx_operand("xg0_1", JH, "plane1_3")
+        make_xq(1, 0, JQ, "bf10")
+        multiply(0, 1)
+        make_xq(0, JH, JH, "bf01")
+        make_xq(1, JQ, JQ, "bf11")
+        multiply(1, 1)
+        multiply(2, 0)
+        value_sum(3, 0)
+        open_unit(0, nc.gpsimd)
+        gate_sum(3, 0)
+        make_xq(1, JH, JQ, "bf12")
+        multiply(2, 1)
+        open_unit(1, nc.gpsimd)
+        make_xq(1, JH + JQ, JQ, "res0")
+        multiply(3, 1)
+        last = len(UNITS) - 1
+        for index in range(2, len(UNITS)):
+            open_unit(index, nc.vector if index == last else nc.gpsimd)
+            close_unit(index - 2, 1)
+            if index in (2, 4):
+                make_vq(index // 2 + 1, 1, "wv%d" % index)
+            if 4 <= index + 2 <= last:
                 for a in range(PASSES):
-                    multiply(unit, a)
-            apply_gate(done)
-            leave_banks(following)
-            sum_and_store(done, UNITS[done])
-        apply_gate((1, 1))
-        sum_and_store((1, 1), [UNITS[1, 1][0], (3, 1, JH, JQ), (3, 1, JH + JQ, JQ)])
+                    gate_sum(index + 2, a)
+                for a in range(PASSES):
+                    value_sum(index + 2, a)
+        close_unit(last - 1, 1)
+        close_unit(last, 2)

@@ -48,7 +48,7 @@ def tile_list_hway_kernel(tc, xT, wgt, wk_words, wk_scales, wv, bg, res, offs, o
         wk_codes = [keep.tile([P, 2 * N], U8, name="wk_codes%d" % a, align_bytes=64) for a in range(PASSES)]
         wk_scale_rows = keep.tile([P, PASSES, N], U8, name="wk_scale_rows", align_bytes=64)
         bias = keep.tile([P, N_TILES], F32, name="bias")
-        wv_raw = [[keep.tile([P, PACK, NH], F32, name="wv_raw%d_%d" % (a, m)) for m in range(2)] for a in range(PASSES)]
+        wv_raw = [[keep.tile([P, PACK, NH], F32, name="wv_raw%d_%d" % (a, m), tag="wv_raw%d_%d" % (a, m), align_bytes=64) for m in range(2)] for a in range(PASSES)]
         res_sb = [keep.tile([P, unit[1], unit[3]], F32, name="res%d" % u, tag="res%d" % u, align_bytes=64) for u, unit in enumerate(UNITS)]
 
         bias_rows = keep.tile([P, P], F32, name="bias_rows")
@@ -108,10 +108,10 @@ def tile_list_hway_kernel(tc, xT, wgt, wk_words, wk_scales, wv, bg, res, offs, o
         nc.sync.dma_start(bias_rows[0:N_TILES, :], bg.rearrange("(c p) -> c p", p=P))
         load_plane(1, 0)
         load_plane(1, 1)
+        load_wk(0)
         load_wv(0, 0)
         load_plane(1, 2)
         load_wv(1, 0)
-        load_wk(0)
         load_plane(1, 3)
         load_wk(1)
         for u in range(4):
@@ -145,25 +145,33 @@ def tile_list_hway_kernel(tc, xT, wgt, wk_words, wk_scales, wv, bg, res, offs, o
         def interleave(grouped, rows):
             nc.scalar.copy(grouped.rearrange("p (c r) i -> p c i r", r=4), rows.rearrange("p i (c r) -> p c i r", r=4))
 
-        def make_xq(a, j0, width, tag):
-            grouped = keep.tile([P, width, PACK], BF16, name="xg_bf%d_%d" % (a, j0), tag=tag, align_bytes=64)
-            interleave(grouped[:], picked[a][:, :, j0:j0 + width])
+        rounded = {}
+
+        def lay_pair(a, i0, j0, width, tag):
+            if i0 == 0:
+                rounded[a, j0] = keep.tile([P, width, PACK], BF16, name="xg_bf%d_%d" % (a, j0), tag=tag, align_bytes=64)
+            nc.scalar.copy(rounded[a, j0][:, :, i0:i0 + 2],
+                           picked[a][:, i0:i0 + 2, j0:j0 + width].rearrange("p i w -> p w i"))
+
+        def make_xq(a, j0, width):
+            lay_pair(a, 2, j0, width, None)
             codes, scales = xq[a, j0 // JH]
             cols = slice(j0 % JH, j0 % JH + width)
             nc.vector.quantize_mx(codes[:, cols].bitcast(FP8X4), scales[:, cols],
-                                  grouped[:].rearrange("p w i -> p (w i)"))
+                                  rounded[a, j0][:].rearrange("p w i -> p (w i)"))
 
-        def make_vq(nt0, count, tag):
+        def make_vq(nt0, count, passes, tag):
+            name = "wv%d_%d" % (nt0, passes[0])
             width = count * P
-            grouped = keep.tile([P, PASSES, width, PACK], BF16, name="wv_bf%d" % nt0, align_bytes=64)
             c0 = (nt0 % 2) * P
-            for a in range(PASSES):
-                interleave(grouped[:, a, :, :], wv_raw[a][nt0 // 2][:, :, c0:c0 + width])
-            codes, scales = mx_operand("wv%d" % nt0, PASSES * width, tag)
+            grouped = keep.tile([P, len(passes), width, PACK], BF16, name=name + "_bf", align_bytes=64)
+            for place, a in enumerate(passes):
+                interleave(grouped[:, place, :, :], wv_raw[a][nt0 // 2][:, :, c0:c0 + width])
+            codes, scales = mx_operand(name, len(passes) * width, tag)
             nc.vector.quantize_mx(codes.bitcast(FP8X4), scales, grouped[:].rearrange("p a w i -> p (a w i)"))
-            for c in range(count):
-                for a in range(PASSES):
-                    cols = slice(a * width + c * P, a * width + (c + 1) * P)
+            for place, a in enumerate(passes):
+                for c in range(count):
+                    cols = slice(place * width + c * P, place * width + (c + 1) * P)
                     vq[a, nt0 + c] = (codes[:, cols], scales[:, cols])
 
         ke_banks = {}
@@ -232,41 +240,49 @@ def tile_list_hway_kernel(tc, xT, wgt, wk_words, wk_scales, wv, bg, res, offs, o
 
         for i in range(PACK):
             gather(0, i, 0, J)
+            if i == 1:
+                for h in range(2):
+                    lay_pair(0, 0, h * JH, JH, "bf0%d" % h)
         gather(1, 0, 0, J)
         gather(1, 1, 0, J)
-        xq[0, 0] = mx_operand("xg0_0", JH, "plane1_1")
-        make_xq(0, 0, JH, "bf00")
+        codes, scales = mx_operand("xg0", J, "plane1_1")
+        for h in range(2):
+            xq[0, h] = (codes[:, h * JH:(h + 1) * JH], scales[:, h * JH:(h + 1) * JH])
+            make_xq(0, h * JH, JH)
         gather(1, 2, 0, J)
-        make_vq(0, 2, "plane1_2")
-        multiply(0, 0)
-        multiply(1, 0)
+        make_vq(0, 2, [0], "plane1_2")
+        for index in range(3):
+            gate_sum(index, 0)
+        for index in range(4):
+            value_sum(index, 0)
+        for q in range(2):
+            lay_pair(1, 0, q * JQ, JQ, "bf1%d" % q)
         for h in range(2):
             xq[1, h] = mx_operand("xg1_%d" % h, JH, "xg1_%d" % h)
 
         gather(1, PACK - 1, 0, JQ)
         gather(1, PACK - 1, JQ, JQ)
         gather(1, PACK - 1, JH, JH)
-        xq[0, 1] = mx_operand("xg0_1", JH, "plane1_3")
-        make_xq(1, 0, JQ, "bf10")
+        make_xq(1, 0, JQ)
+        make_vq(0, 2, [1], "plane1_3")
+        lay_pair(1, 0, 2 * JQ, JQ, "bf12")
+        lay_pair(1, 0, 3 * JQ, JQ, "wv_raw1_0")
         multiply(0, 1)
-        make_xq(0, JH, JH, "bf01")
-        make_xq(1, JQ, JQ, "bf11")
+        make_xq(1, JQ, JQ)
         multiply(1, 1)
-        multiply(2, 0)
-        value_sum(3, 0)
-        open_unit(0, nc.gpsimd)
-        gate_sum(3, 0)
-        make_xq(1, JH, JQ, "bf12")
+        make_xq(1, JH, JQ)
         multiply(2, 1)
+        open_unit(0, nc.vector)
+        gate_sum(3, 0)
         open_unit(1, nc.gpsimd)
-        make_xq(1, JH + JQ, JQ, "res0")
+        make_xq(1, JH + JQ, JQ)
         multiply(3, 1)
         last = len(UNITS) - 1
         for index in range(2, len(UNITS)):
             open_unit(index, nc.vector if index == last else nc.gpsimd)
             close_unit(index - 2, 1)
             if index in (2, 4):
-                make_vq(index // 2 + 1, 1, "wv%d" % index)
+                make_vq(index // 2 + 1, 1, [0, 1], "wv%d" % index)
             if 4 <= index + 2 <= last:
                 for a in range(PASSES):
                     gate_sum(index + 2, a)

@@ -114,11 +114,11 @@ def tile_list_hway_kernel(tc, xT, wgt, wk_words, wk_scales, wv, bg, res, offs, o
         load_wv(1, 0)
         load_plane(1, 3)
         load_wk(1)
-        for u in range(4):
+        for u in range(2):
             load_res(u)
         load_wv(0, 1)
         load_wv(1, 1)
-        for u in range(4, 8):
+        for u in range(2, 8):
             load_res(u)
 
         bias_turned = psum.tile([P, P], F32, name="ke", bufs=3)
@@ -145,30 +145,30 @@ def tile_list_hway_kernel(tc, xT, wgt, wk_words, wk_scales, wv, bg, res, offs, o
         def interleave(grouped, rows):
             nc.scalar.copy(grouped.rearrange("p (c r) i -> p c i r", r=4), rows.rearrange("p i (c r) -> p c i r", r=4))
 
-        rounded = {}
+        def lay_pair(rounded, a, i0, j0, width):
+            nc.scalar.copy(rounded[:, :, i0:i0 + 2], picked[a][:, i0:i0 + 2, j0:j0 + width].rearrange("p i w -> p w i"))
 
-        def lay_pair(a, i0, j0, width, tag):
-            if i0 == 0:
-                rounded[a, j0] = keep.tile([P, width, PACK], BF16, name="xg_bf%d_%d" % (a, j0), tag=tag, align_bytes=64)
-            nc.scalar.copy(rounded[a, j0][:, :, i0:i0 + 2],
-                           picked[a][:, i0:i0 + 2, j0:j0 + width].rearrange("p i w -> p w i"))
-
-        def make_xq(a, j0, width):
-            lay_pair(a, 2, j0, width, None)
+        def make_xq(rounded, a, j0, width):
             codes, scales = xq[a, j0 // JH]
             cols = slice(j0 % JH, j0 % JH + width)
-            nc.vector.quantize_mx(codes[:, cols].bitcast(FP8X4), scales[:, cols],
-                                  rounded[a, j0][:].rearrange("p w i -> p (w i)"))
+            nc.vector.quantize_mx(codes[:, cols].bitcast(FP8X4), scales[:, cols], rounded.rearrange("p w i -> p (w i)"))
 
-        def make_vq(nt0, count, passes, tag):
-            name = "wv%d_%d" % (nt0, passes[0])
+        wv_bf = {}
+
+        def round_wv(nt0, count, passes):
             width = count * P
             c0 = (nt0 % 2) * P
-            grouped = keep.tile([P, len(passes), width, PACK], BF16, name=name + "_bf", align_bytes=64)
+            grouped = keep.tile([P, len(passes), width, PACK], BF16, name="wv_bf%d_%d" % (nt0, passes[0]),
+                                align_bytes=64)
+            wv_bf[nt0, passes[0]] = grouped
             for place, a in enumerate(passes):
                 interleave(grouped[:, place, :, :], wv_raw[a][nt0 // 2][:, :, c0:c0 + width])
-            codes, scales = mx_operand(name, len(passes) * width, tag)
-            nc.vector.quantize_mx(codes.bitcast(FP8X4), scales, grouped[:].rearrange("p a w i -> p (a w i)"))
+
+        def make_vq(nt0, count, passes, operand):
+            width = count * P
+            codes, scales = operand
+            nc.vector.quantize_mx(codes.bitcast(FP8X4), scales,
+                                  wv_bf[nt0, passes[0]][:].rearrange("p a w i -> p (a w i)"))
             for place, a in enumerate(passes):
                 for c in range(count):
                     cols = slice(place * width + c * P, place * width + (c + 1) * P)
@@ -215,22 +215,31 @@ def tile_list_hway_kernel(tc, xT, wgt, wk_words, wk_scales, wv, bg, res, offs, o
             value_sum(index, a)
 
         diffs = {}
+        rests = {}
 
-        def open_unit(index, engine):
+        def open_unit(index):
             nt0, count, j0, width = UNITS[index]
             ke, ve = ke_banks[index], ve_banks[index]
             rest = work.tile([P, count, width], F32, name="rest")
-            diff = work.tile([P, count, width], F32, name="diff", bufs=4)
-            diffs[index] = diff
+            diff = work.tile([P, count, width], F32, name="diff")
+            diffs[index] = diff[:]
+            rests[index] = rest[:]
             for c in range(count):
                 nc.scalar.activation(rest[:, c, :], ke[:, c, :], ACT.Sigmoid,
                                      bias=bias[:, nt0 + c:nt0 + c + 1], scale=-1.0)
             nc.vector.tensor_tensor(diff[:], ve[:], res_sb[index][:], ALU.subtract)
-            engine.tensor_tensor(diff[:], diff[:], rest[:], ALU.mult)
 
-        def close_unit(index, pieces):
+        def gate_on_gpsimd(index):
+            nc.gpsimd.tensor_tensor(diffs[index], diffs[index], rests[index], ALU.mult)
+
+        def gate_on_vector(index, words):
+            product = words.bitcast(F32).rearrange("p (c w) -> p c w", c=UNITS[index][1])
+            nc.vector.tensor_tensor(product, diffs[index], rests[index], ALU.mult)
+            diffs[index] = product
+
+        def close_unit(index, pieces, tag):
             nt0, count, j0, width = UNITS[index]
-            result = keep.tile([P, count, width], F32, name="result%d" % index, tag="res%d" % (index + 1), align_bytes=64)
+            result = keep.tile([P, count, width], F32, name="result%d" % index, tag=tag, align_bytes=64)
             step = width // pieces
             for c0 in range(0, width, step):
                 cols = slice(c0, c0 + step)
@@ -238,55 +247,67 @@ def tile_list_hway_kernel(tc, xT, wgt, wk_words, wk_scales, wv, bg, res, offs, o
                                         ALU.subtract)
                 nc.sync.dma_start(unit_of(out, index)[:, :, cols], result[:, :, cols])
 
+        def both_passes(index):
+            for a in range(PASSES):
+                gate_sum(index, a)
+            for a in range(PASSES):
+                value_sum(index, a)
+
+        early = [keep.tile([P, JH, PACK], BF16, name="early%d" % h, align_bytes=64) for h in range(2)]
         for i in range(PACK):
             gather(0, i, 0, J)
-            if i == 1:
+            if i % 2 == 1:
                 for h in range(2):
-                    lay_pair(0, 0, h * JH, JH, "bf0%d" % h)
+                    lay_pair(early[h][:], 0, i - 1, h * JH, JH)
         gather(1, 0, 0, J)
         gather(1, 1, 0, J)
         codes, scales = mx_operand("xg0", J, "plane1_1")
         for h in range(2):
             xq[0, h] = (codes[:, h * JH:(h + 1) * JH], scales[:, h * JH:(h + 1) * JH])
-            make_xq(0, h * JH, JH)
+            make_xq(early[h][:], 0, h * JH, JH)
         gather(1, 2, 0, J)
-        make_vq(0, 2, [0], "plane1_2")
+        round_wv(0, 2, [0])
+        make_vq(0, 2, [0], mx_operand("wv0_0", NH, "plane1_2"))
         for index in range(3):
             gate_sum(index, 0)
         for index in range(4):
             value_sum(index, 0)
-        for q in range(2):
-            lay_pair(1, 0, q * JQ, JQ, "bf1%d" % q)
+        late = keep.tile([P, J, PACK], BF16, name="late", tag="wv_raw0_0", align_bytes=64)
+        lay_pair(late[:], 1, 0, 0, J)
+        round_wv(0, 2, [1])
         for h in range(2):
             xq[1, h] = mx_operand("xg1_%d" % h, JH, "xg1_%d" % h)
 
         gather(1, PACK - 1, 0, JQ)
         gather(1, PACK - 1, JQ, JQ)
         gather(1, PACK - 1, JH, JH)
-        make_xq(1, 0, JQ)
-        make_vq(0, 2, [1], "plane1_3")
-        lay_pair(1, 0, 2 * JQ, JQ, "bf12")
-        lay_pair(1, 0, 3 * JQ, JQ, "wv_raw1_0")
-        multiply(0, 1)
-        make_xq(1, JQ, JQ)
-        multiply(1, 1)
-        make_xq(1, JH, JQ)
-        multiply(2, 1)
-        open_unit(0, nc.vector)
-        gate_sum(3, 0)
-        open_unit(1, nc.gpsimd)
-        make_xq(1, JH + JQ, JQ)
-        multiply(3, 1)
+        for q in range(4):
+            piece = late[:, q * JQ:(q + 1) * JQ, :]
+            lay_pair(piece, 1, 2, q * JQ, JQ)
+            make_xq(piece, 1, q * JQ, JQ)
+            if q == 0:
+                make_vq(0, 2, [1], mx_operand("wv0_1", NH, "plane1_3"))
+            if q < 3:
+                gate_sum(q, 1)
+            value_sum(q, 1)
+        open_unit(0)
+        gate_on_vector(0, keep.tile([P, JH], U32, name="product0")[:])
+        for a in range(PASSES):
+            gate_sum(3, a)
+        open_unit(1)
+        gate_on_gpsimd(1)
         last = len(UNITS) - 1
         for index in range(2, len(UNITS)):
-            open_unit(index, nc.vector if index == last else nc.gpsimd)
-            close_unit(index - 2, 1)
+            open_unit(index)
+            if index != last - 1:
+                gate_on_gpsimd(index)
+            if index == last:
+                gate_on_vector(last - 1, keep.tile([P, JH], U32, name="product6", tag="res7", align_bytes=64)[:])
+            close_unit(index - 2, 1, "res%d" % (index - 1))
             if index in (2, 4):
-                make_vq(index // 2 + 1, 1, [0, 1], "wv%d" % index)
+                round_wv(index // 2 + 1, 1, [0, 1])
+                make_vq(index // 2 + 1, 1, [0, 1], mx_operand("wv%d" % index, NH, "wv%d" % index))
             if 4 <= index + 2 <= last:
-                for a in range(PASSES):
-                    gate_sum(index + 2, a)
-                for a in range(PASSES):
-                    value_sum(index + 2, a)
-        close_unit(last - 1, 1)
-        close_unit(last, 2)
+                both_passes(index + 2)
+        close_unit(last - 1, 1, "result6")
+        close_unit(last, 2, "result7")

@@ -291,23 +291,36 @@ def tile_list_hway_kernel(tc, xT, wgt, wk_words, wk_scales, wv, bg, res, offs, o
                 gate_sum(q, 1)
             value_sum(q, 1)
         open_unit(0)
-        gate_on_vector(0, keep.tile([P, JH], U32, name="product0")[:])
         for a in range(PASSES):
             gate_sum(3, a)
         open_unit(1)
-        gate_on_gpsimd(1)
-        last = len(UNITS) - 1
-        for index in range(2, len(UNITS)):
-            open_unit(index)
-            if index != last - 1:
-                gate_on_gpsimd(index)
-            if index == last:
-                gate_on_vector(last - 1, keep.tile([P, JH], U32, name="product6", tag="res7", align_bytes=64)[:])
-            close_unit(index - 2, 1, "res%d" % (index - 1))
-            if index in (2, 4):
-                round_wv(index // 2 + 1, 1, [0, 1])
-                make_vq(index // 2 + 1, 1, [0, 1], mx_operand("wv%d" % index, NH, "wv%d" % index))
-            if 4 <= index + 2 <= last:
-                both_passes(index + 2)
-        close_unit(last - 1, 1, "result6")
-        close_unit(last, 2, "result7")
+        open_unit(2)
+        for index in range(2):
+            gate_on_vector(index, keep.tile([P, JH], U32, name="product%d" % index)[:])
+        gate_on_gpsimd(2)
+        round_wv(2, 1, [0, 1])
+        open_unit(3)
+        gate_on_gpsimd(3)
+        close_unit(0, 1, "res1")
+        make_vq(2, 1, [0, 1], mx_operand("wv2", NH, "wv2"))
+        both_passes(4)
+        close_unit(1, 1, "res2")
+        both_passes(5)
+        round_wv(3, 1, [0, 1])
+        open_unit(4)
+        gate_on_gpsimd(4)
+        close_unit(2, 1, "res3")
+        make_vq(3, 1, [0, 1], mx_operand("wv3", NH, "wv3"))
+        both_passes(6)
+        open_unit(5)
+        gate_on_gpsimd(5)
+        close_unit(3, 1, "res4")
+        both_passes(7)
+        open_unit(6)
+        close_unit(4, 1, "res5")
+        open_unit(7)
+        gate_on_gpsimd(7)
+        gate_on_vector(6, keep.tile([P, JH], U32, name="product6", tag="res7", align_bytes=64)[:])
+        close_unit(5, 1, "res6")
+        close_unit(6, 1, "result6")
+        close_unit(7, 2, "result7")

@@ -29,9 +29,11 @@ JH = 512
 JQ = 256
 NH = 256
 N_TILES = N // P
+KE_BANK = [0, 1, 2, 7, 0, 2, 0, 2]
+VE_BANK = [3, 4, 5, 6, 1, 3, 4, 5]
+TURN_BANK = 7
 
-UNITS = [(0, 2, 0, JQ), (0, 2, JQ, JQ), (0, 2, JH, JQ), (0, 2, JH + JQ, JQ),
-         (2, 1, 0, JH), (2, 1, JH, JH), (3, 1, 0, JH), (3, 1, JH, JH)]
+UNITS = [(0, 2, q * JQ, JQ) for q in range(4)] + [(nt, 1, h * JH, JH) for nt in (2, 3) for h in range(2)]
 
 
 def tile_list_hway_kernel(tc, xT, wgt, wk_words, wk_scales, wv, bg, res, offs, out):
@@ -39,7 +41,10 @@ def tile_list_hway_kernel(tc, xT, wgt, wk_words, wk_scales, wv, bg, res, offs, o
     with ExitStack() as ctx:
         keep = ctx.enter_context(tc.tile_pool(name="keep", bufs=1))
         work = ctx.enter_context(tc.tile_pool(name="work", bufs=4))
-        psum = ctx.enter_context(tc.psum_pool(name="psum", bufs=4))
+        psum = ctx.enter_context(tc.psum_pool(name="psum", bufs=1))
+
+        def bank(shape, number):
+            return psum.tile(shape, F32, name="bank%d" % number)
 
         offsets = keep.tile([P, J // GROUP], U16, name="offsets")
         weights = keep.tile([P, J], F32, name="weights", align_bytes=64)
@@ -47,9 +52,10 @@ def tile_list_hway_kernel(tc, xT, wgt, wk_words, wk_scales, wv, bg, res, offs, o
                    for i in range(PACK)] for a in range(PASSES)]
         wk_codes = [keep.tile([P, 2 * N], U8, name="wk_codes%d" % a, align_bytes=64) for a in range(PASSES)]
         wk_scale_rows = keep.tile([P, PASSES, N], U8, name="wk_scale_rows", align_bytes=64)
-        bias = keep.tile([P, N_TILES], F32, name="bias")
-        wv_raw = [[keep.tile([P, PACK, NH], F32, name="wv_raw%d_%d" % (a, m), tag="wv_raw%d_%d" % (a, m), align_bytes=64) for m in range(2)] for a in range(PASSES)]
-        res_sb = [keep.tile([P, unit[1], unit[3]], F32, name="res%d" % u, tag="res%d" % u, align_bytes=64) for u, unit in enumerate(UNITS)]
+        wv_raw = [[keep.tile([P, PACK, NH], F32, name="wv_raw%d_%d" % (a, m), tag="wv_raw%d_%d" % (a, m), align_bytes=64)
+                   for m in range(2)] for a in range(PASSES)]
+        res_sb = [keep.tile([P, unit[1], unit[3]], F32, name="res%d" % u, tag="res%d" % u, align_bytes=64)
+                  for u, unit in enumerate(UNITS)]
 
         bias_rows = keep.tile([P, P], F32, name="bias_rows")
         identity = keep.tile([P, P], F32, name="identity")
@@ -97,9 +103,8 @@ def tile_list_hway_kernel(tc, xT, wgt, wk_words, wk_scales, wv, bg, res, offs, o
             nc.vector.transpose(weights[:, h * JH:(h + 1) * JH],
                                 w_spread[:, b, :, :].rearrange("p b g r -> p (b g r)"))
 
-        load_plane(0, 1)
-        load_plane(0, 2)
-        load_plane(0, 3)
+        for i in range(1, PACK):
+            load_plane(0, i)
         for q in range(P // QUAD):
             nc.sync.dma_start(
                 wk_scale_rows[QUAD * q:QUAD * q + 4, :, :].bitcast(I32),
@@ -114,16 +119,19 @@ def tile_list_hway_kernel(tc, xT, wgt, wk_words, wk_scales, wv, bg, res, offs, o
         load_wv(1, 0)
         load_plane(1, 3)
         load_wk(1)
-        for u in range(2):
-            load_res(u)
+        load_res(0)
+        load_res(1)
         load_wv(0, 1)
         load_wv(1, 1)
-        for u in range(2, 8):
+        for u in range(2, len(UNITS)):
             load_res(u)
 
-        bias_turned = psum.tile([P, P], F32, name="ke", bufs=3)
+        bias = keep.tile([P, N_TILES], F32, name="bias")
+        minus_bias = keep.tile([P, N_TILES], F32, name="minus_bias")
+        bias_turned = bank([P, P], 0)
         nc.tensor.transpose(bias_turned[:], bias_rows[:], identity[:])
-        nc.scalar.mul(bias[:], bias_turned[:, 0:N_TILES], -1.0)
+        nc.scalar.copy(bias[:], bias_turned[:, 0:N_TILES])
+        nc.scalar.mul(minus_bias[:], bias_turned[:, 0:N_TILES], -1.0)
 
         picked = [keep.tile([P, PACK, J], F32, name="picked%d" % a) for a in range(PASSES)]
         xq = {}
@@ -142,16 +150,13 @@ def tile_list_hway_kernel(tc, xT, wgt, wk_words, wk_scales, wv, bg, res, offs, o
                 ALU.mult,
             )
 
-        def interleave(grouped, rows):
-            nc.scalar.copy(grouped.rearrange("p (c r) i -> p c i r", r=4), rows.rearrange("p i (c r) -> p c i r", r=4))
-
         def lay_pair(rounded, a, i0, j0, width):
             nc.scalar.copy(rounded[:, :, i0:i0 + 2], picked[a][:, i0:i0 + 2, j0:j0 + width].rearrange("p i w -> p w i"))
 
         def make_xq(rounded, a, j0, width):
-            codes, scales = xq[a, j0 // JH]
-            cols = slice(j0 % JH, j0 % JH + width)
-            nc.vector.quantize_mx(codes[:, cols].bitcast(FP8X4), scales[:, cols], rounded.rearrange("p w i -> p (w i)"))
+            codes, scales = xq[a]
+            nc.vector.quantize_mx(codes[:, j0:j0 + width].bitcast(FP8X4), scales[:, j0:j0 + width],
+                                  rounded.rearrange("p w i -> p (w i)"))
 
         wv_bf = {}
 
@@ -162,11 +167,12 @@ def tile_list_hway_kernel(tc, xT, wgt, wk_words, wk_scales, wv, bg, res, offs, o
                                 align_bytes=64)
             wv_bf[nt0, passes[0]] = grouped
             for place, a in enumerate(passes):
-                interleave(grouped[:, place, :, :], wv_raw[a][nt0 // 2][:, :, c0:c0 + width])
+                nc.scalar.copy(grouped[:, place, :, :].rearrange("p (c r) i -> p c i r", r=4),
+                               wv_raw[a][nt0 // 2][:, :, c0:c0 + width].rearrange("p i (c r) -> p c i r", r=4))
 
-        def make_vq(nt0, count, passes, operand):
+        def make_vq(nt0, count, passes, tag):
             width = count * P
-            codes, scales = operand
+            codes, scales = mx_operand("wv%d_%d" % (nt0, passes[0]), len(passes) * width, tag)
             nc.vector.quantize_mx(codes.bitcast(FP8X4), scales,
                                   wv_bf[nt0, passes[0]][:].rearrange("p a w i -> p (a w i)"))
             for place, a in enumerate(passes):
@@ -177,81 +183,123 @@ def tile_list_hway_kernel(tc, xT, wgt, wk_words, wk_scales, wv, bg, res, offs, o
         ke_banks = {}
         ve_banks = {}
 
-        def gate_sum(index, a):
-            nt0, count, j0, width = UNITS[index]
+        def gate_sum(u, a):
+            nt0, count, j0, width = UNITS[u]
             if a == 0:
-                ke_banks[index] = psum.tile([P, count, width], F32, name="ke", bufs=3)
-            ke = ke_banks[index]
-            x_codes, x_scales = xq[a, j0 // JH]
-            c0 = j0 % JH
+                ke_banks[u] = bank([P, count, width], KE_BANK[u])
+            x_codes, x_scales = xq[a]
             step = JH if width == JH else P
-            for u in range(count):
-                nt = nt0 + u
+            for c in range(count):
+                nt = nt0 + c
                 for b in range(0, width, step):
+                    cols = slice(j0 + b, j0 + b + step)
                     nc.tensor.matmul_mx(
-                        ke[:, u, b:b + step], lhsT=wk_codes[a][:, 2 * P * nt:2 * P * (nt + 1)].bitcast(FP4X4),
+                        ke_banks[u][:, c, b:b + step], lhsT=wk_codes[a][:, 2 * P * nt:2 * P * (nt + 1)].bitcast(FP4X4),
                         lhsT_scale=wk_scale_rows[:, a, P * nt:P * (nt + 1)],
-                        rhs=x_codes[:, c0 + b:c0 + b + step].bitcast(FP8X4),
-                        rhs_scale=x_scales[:, c0 + b:c0 + b + step],
-                        start=(a == 0 and u == 0 and b == 0),
-                        stop=(a == PASSES - 1 and u == count - 1 and b + step == width))
+                        rhs=x_codes[:, cols].bitcast(FP8X4), rhs_scale=x_scales[:, cols],
+                        start=(a == 0 and c == 0 and b == 0),
+                        stop=(a == PASSES - 1 and c == count - 1 and b + step == width))
 
-        def value_sum(index, a):
-            nt0, count, j0, width = UNITS[index]
+        def value_sum(u, a):
+            nt0, count, j0, width = UNITS[u]
             if a == 0:
-                ve_banks[index] = psum.tile([P, count, width], F32, name="ve", bufs=5)
-            ve = ve_banks[index]
-            x_codes, x_scales = xq[a, j0 // JH]
-            c0 = j0 % JH
-            for u in range(count):
-                v_codes, v_scales = vq[a, nt0 + u]
+                ve_banks[u] = bank([P, count, width], VE_BANK[u])
+            x_codes, x_scales = xq[a]
+            for c in range(count):
+                v_codes, v_scales = vq[a, nt0 + c]
                 nc.tensor.matmul_mx(
-                    ve[:, u, :], lhsT=v_codes.bitcast(FP8X4), lhsT_scale=v_scales,
-                    rhs=x_codes[:, c0:c0 + width].bitcast(FP8X4), rhs_scale=x_scales[:, c0:c0 + width],
-                    start=(a == 0 and u == 0), stop=(a == PASSES - 1 and u == count - 1))
-
-        def multiply(index, a):
-            gate_sum(index, a)
-            value_sum(index, a)
+                    ve_banks[u][:, c, :], lhsT=v_codes.bitcast(FP8X4), lhsT_scale=v_scales,
+                    rhs=x_codes[:, j0:j0 + width].bitcast(FP8X4), rhs_scale=x_scales[:, j0:j0 + width],
+                    start=(a == 0 and c == 0), stop=(a == PASSES - 1 and c == count - 1))
 
         diffs = {}
+
         rests = {}
 
-        def open_unit(index):
-            nt0, count, j0, width = UNITS[index]
-            ke, ve = ke_banks[index], ve_banks[index]
+        def gate_on_vector(u, tag):
+            product = keep.tile([P, 1, JH], F32, name="product%d" % u, tag=tag, align_bytes=64)
+            nc.vector.tensor_tensor(product[:], diffs[u][:], rests[u][:], ALU.mult)
+            diffs[u] = product
+
+        def open_unit(u, on_gpsimd=True):
+            nt0, count, j0, width = UNITS[u]
             rest = work.tile([P, count, width], F32, name="rest")
-            diff = work.tile([P, count, width], F32, name="diff")
-            diffs[index] = diff[:]
-            rests[index] = rest[:]
+            diffs[u] = work.tile([P, count, width], F32, name="diff")
             for c in range(count):
-                nc.scalar.activation(rest[:, c, :], ke[:, c, :], ACT.Sigmoid,
-                                     bias=bias[:, nt0 + c:nt0 + c + 1], scale=-1.0)
-            nc.vector.tensor_tensor(diff[:], ve[:], res_sb[index][:], ALU.subtract)
+                nc.scalar.activation(rest[:, c, :], ke_banks[u][:, c, :], ACT.Sigmoid,
+                                     bias=minus_bias[:, nt0 + c:nt0 + c + 1], scale=-1.0)
+            nc.vector.tensor_tensor(diffs[u][:], ve_banks[u][:], res_sb[u][:], ALU.subtract)
+            rests[u] = rest
+            if on_gpsimd:
+                nc.gpsimd.tensor_tensor(diffs[u][:], diffs[u][:], rest[:], ALU.mult)
 
-        def gate_on_gpsimd(index):
-            nc.gpsimd.tensor_tensor(diffs[index], diffs[index], rests[index], ALU.mult)
-
-        def gate_on_vector(index, words):
-            product = words.bitcast(F32).rearrange("p (c w) -> p c w", c=UNITS[index][1])
-            nc.vector.tensor_tensor(product, diffs[index], rests[index], ALU.mult)
-            diffs[index] = product
-
-        def close_unit(index, pieces, tag):
-            nt0, count, j0, width = UNITS[index]
-            result = keep.tile([P, count, width], F32, name="result%d" % index, tag=tag, align_bytes=64)
+        def close_unit(u, pieces, tag):
+            nt0, count, j0, width = UNITS[u]
+            result = keep.tile([P, count, width], F32, name="result%d" % u, tag=tag, align_bytes=64)
             step = width // pieces
             for c0 in range(0, width, step):
                 cols = slice(c0, c0 + step)
-                nc.vector.tensor_tensor(result[:, :, cols], ve_banks[index][:, :, cols], diffs[index][:, :, cols],
-                                        ALU.subtract)
-                nc.sync.dma_start(unit_of(out, index)[:, :, cols], result[:, :, cols])
+                nc.vector.tensor_tensor(result[:, :, cols], ve_banks[u][:, :, cols], diffs[u][:, :, cols], ALU.subtract)
+                nc.sync.dma_start(unit_of(out, u)[:, :, cols], result[:, :, cols])
 
-        def both_passes(index):
+        blocks = JH // P
+        res_turned = {}
+        gate_turned = {}
+        diff_turned = {}
+
+        def turn(source):
+            turned = bank([P, blocks, P], TURN_BANK)
+            for b in range(blocks):
+                nc.tensor.transpose(turned[:, b, :], source[:, b * P:(b + 1) * P], identity[:])
+            return turned
+
+        def turn_res(u):
+            res_turned[u] = keep.tile([P, blocks, P], F32, name="res_turned%d" % u)
+            nc.scalar.copy(res_turned[u][:], turn(res_sb[u][:, 0, :])[:])
+
+        def turned_value_sum(u):
+            nt, count, j0, width = UNITS[u]
+            ve_banks[u] = bank([P, blocks, P], VE_BANK[u])
+            for b in range(blocks):
+                cols = slice(j0 + b * P, j0 + (b + 1) * P)
+                for a in range(PASSES):
+                    x_codes, x_scales = xq[a]
+                    v_codes, v_scales = vq[a, nt]
+                    nc.tensor.matmul_mx(
+                        ve_banks[u][:, b, :], lhsT=x_codes[:, cols].bitcast(FP8X4), lhsT_scale=x_scales[:, cols],
+                        rhs=v_codes.bitcast(FP8X4), rhs_scale=v_scales, start=(a == 0), stop=(a == PASSES - 1))
+
+        def open_turned(u):
+            nt = UNITS[u][0]
+            gate = keep.tile([P, JH], F32, name="gate%d" % u)
+            nc.scalar.activation(gate[:], ke_banks[u][:, 0, :], ACT.Sigmoid, bias=bias[:, nt:nt + 1])
+            gate_turned[u] = turn(gate[:])
+            diff_turned[u] = keep.tile([P, blocks, P], F32, name="diff_turned%d" % u, tag="diff_turned", align_bytes=64)
+            nc.vector.tensor_tensor(diff_turned[u][:], ve_banks[u][:], res_turned[u][:], ALU.subtract)
+
+        def gate_turned_unit(u):
+            gated = keep.tile([P, blocks, P], F32, name="gated%d" % u)
+            nc.vector.tensor_tensor(gated[:], gate_turned[u][:], diff_turned[u][:], ALU.mult)
+            diff_turned[u] = gated
+
+        def close_turned(u):
+            total = bank([P, blocks, P], VE_BANK[u])
+            for b in range(blocks):
+                nc.tensor.matmul(total[:, b, :], res_turned[u][:, b, :], identity[:], start=True, stop=False,
+                                 is_transpose=True)
+                nc.tensor.matmul(total[:, b, :], diff_turned[u][:, b, :], identity[:], start=False, stop=True,
+                                 is_transpose=True)
+            result = keep.tile([P, blocks, P], F32, name="result%d" % u)
+            nc.scalar.copy(result[:], total[:])
+            nc.sync.dma_start(unit_of(out, u)[:, 0, :], result[:].rearrange("p b j -> p (b j)"))
+
+        def gate_sums(u):
             for a in range(PASSES):
-                gate_sum(index, a)
+                gate_sum(u, a)
+
+        def value_sums(u):
             for a in range(PASSES):
-                value_sum(index, a)
+                value_sum(u, a)
 
         early = [keep.tile([P, JH, PACK], BF16, name="early%d" % h, align_bytes=64) for h in range(2)]
         for i in range(PACK):
@@ -261,22 +309,20 @@ def tile_list_hway_kernel(tc, xT, wgt, wk_words, wk_scales, wv, bg, res, offs, o
                     lay_pair(early[h][:], 0, i - 1, h * JH, JH)
         gather(1, 0, 0, J)
         gather(1, 1, 0, J)
-        codes, scales = mx_operand("xg0", J, "plane1_1")
+        xq[0] = mx_operand("xg0", J, "plane1_1")
         for h in range(2):
-            xq[0, h] = (codes[:, h * JH:(h + 1) * JH], scales[:, h * JH:(h + 1) * JH])
             make_xq(early[h][:], 0, h * JH, JH)
         gather(1, 2, 0, J)
         round_wv(0, 2, [0])
-        make_vq(0, 2, [0], mx_operand("wv0_0", NH, "plane1_2"))
-        for index in range(3):
-            gate_sum(index, 0)
-        for index in range(4):
-            value_sum(index, 0)
+        make_vq(0, 2, [0], "plane1_2")
+        for u in range(4):
+            gate_sum(u, 0)
+        for u in range(4):
+            value_sum(u, 0)
         late = keep.tile([P, J, PACK], BF16, name="late", tag="wv_raw0_0", align_bytes=64)
         lay_pair(late[:], 1, 0, 0, J)
         round_wv(0, 2, [1])
-        for h in range(2):
-            xq[1, h] = mx_operand("xg1_%d" % h, JH, "xg1_%d" % h)
+        xq[1] = mx_operand("xg1", J, "xg1")
 
         gather(1, PACK - 1, 0, JQ)
         gather(1, PACK - 1, JQ, JQ)
@@ -286,41 +332,37 @@ def tile_list_hway_kernel(tc, xT, wgt, wk_words, wk_scales, wv, bg, res, offs, o
             lay_pair(piece, 1, 2, q * JQ, JQ)
             make_xq(piece, 1, q * JQ, JQ)
             if q == 0:
-                make_vq(0, 2, [1], mx_operand("wv0_1", NH, "plane1_3"))
-            if q < 3:
-                gate_sum(q, 1)
+                make_vq(0, 2, [1], "plane1_3")
+            gate_sum(q, 1)
             value_sum(q, 1)
         open_unit(0)
-        for a in range(PASSES):
-            gate_sum(3, a)
         open_unit(1)
         open_unit(2)
-        for index in range(2):
-            gate_on_vector(index, keep.tile([P, JH], U32, name="product%d" % index)[:])
-        gate_on_gpsimd(2)
         round_wv(2, 1, [0, 1])
-        open_unit(3)
-        gate_on_gpsimd(3)
         close_unit(0, 1, "res1")
-        make_vq(2, 1, [0, 1], mx_operand("wv2", NH, "wv2"))
-        both_passes(4)
-        close_unit(1, 1, "res2")
-        both_passes(5)
+        make_vq(2, 1, [0, 1], "wv2")
+        gate_sums(4)
+        value_sums(4)
+        open_unit(3)
+        gate_sums(5)
+        value_sums(5)
         round_wv(3, 1, [0, 1])
+        close_unit(1, 1, "res2")
+        make_vq(3, 1, [0, 1], "wv3")
         open_unit(4)
-        gate_on_gpsimd(4)
+        gate_sums(6)
+        turn_res(6)
+        turned_value_sum(6)
         close_unit(2, 1, "res3")
-        make_vq(3, 1, [0, 1], mx_operand("wv3", NH, "wv3"))
-        both_passes(6)
-        open_unit(5)
-        gate_on_gpsimd(5)
+        open_turned(6)
+        value_sums(7)
+        open_unit(5, False)
+        gate_sums(7)
         close_unit(3, 1, "res4")
-        both_passes(7)
-        open_unit(6)
-        close_unit(4, 1, "res5")
         open_unit(7)
-        gate_on_gpsimd(7)
-        gate_on_vector(6, keep.tile([P, JH], U32, name="product6", tag="res7", align_bytes=64)[:])
-        close_unit(5, 1, "res6")
-        close_unit(6, 1, "result6")
+        gate_turned_unit(6)
+        gate_on_vector(5, "res7")
+        close_turned(6)
+        close_unit(4, 1, "res5")
+        close_unit(5, 1, "result5")
         close_unit(7, 2, "result7")

@@ -29,9 +29,8 @@ JH = 512
 JQ = 256
 NH = 256
 N_TILES = N // P
-KE_BANK = [0, 1, 2, 7, 0, 2, 0, 2]
+KE_BANK = [0, 1, 2, 7, 0, 2, 7, 0]
 VE_BANK = [3, 4, 5, 6, 1, 3, 4, 5]
-TURN_BANK = 7
 
 UNITS = [(0, 2, q * JQ, JQ) for q in range(4)] + [(nt, 1, h * JH, JH) for nt in (2, 3) for h in range(2)]
 
@@ -126,11 +125,9 @@ def tile_list_hway_kernel(tc, xT, wgt, wk_words, wk_scales, wv, bg, res, offs, o
         for u in range(2, len(UNITS)):
             load_res(u)
 
-        bias = keep.tile([P, N_TILES], F32, name="bias")
         minus_bias = keep.tile([P, N_TILES], F32, name="minus_bias")
         bias_turned = bank([P, P], 0)
         nc.tensor.transpose(bias_turned[:], bias_rows[:], identity[:])
-        nc.scalar.copy(bias[:], bias_turned[:, 0:N_TILES])
         nc.scalar.mul(minus_bias[:], bias_turned[:, 0:N_TILES], -1.0)
 
         picked = [keep.tile([P, PACK, J], F32, name="picked%d" % a) for a in range(PASSES)]
@@ -154,8 +151,9 @@ def tile_list_hway_kernel(tc, xT, wgt, wk_words, wk_scales, wv, bg, res, offs, o
             nc.scalar.copy(rounded[:, :, i0:i0 + 2], picked[a][:, i0:i0 + 2, j0:j0 + width].rearrange("p i w -> p w i"))
 
         def make_xq(rounded, a, j0, width):
-            codes, scales = xq[a]
-            nc.vector.quantize_mx(codes[:, j0:j0 + width].bitcast(FP8X4), scales[:, j0:j0 + width],
+            codes, scales = xq[a, j0 // JH]
+            c0 = j0 % JH
+            nc.vector.quantize_mx(codes[:, c0:c0 + width].bitcast(FP8X4), scales[:, c0:c0 + width],
                                   rounded.rearrange("p w i -> p (w i)"))
 
         wv_bf = {}
@@ -163,7 +161,7 @@ def tile_list_hway_kernel(tc, xT, wgt, wk_words, wk_scales, wv, bg, res, offs, o
         def round_wv(nt0, count, passes):
             width = count * P
             c0 = (nt0 % 2) * P
-            grouped = keep.tile([P, len(passes), width, PACK], BF16, name="wv_bf%d_%d" % (nt0, passes[0]),
+            grouped = keep.tile([P, len(passes), width, PACK], BF16, name="wv_bf%d_%d" % (nt0, passes[0]), tag="wv_bf%d_%d" % (nt0, passes[0]),
                                 align_bytes=64)
             wv_bf[nt0, passes[0]] = grouped
             for place, a in enumerate(passes):
@@ -187,7 +185,8 @@ def tile_list_hway_kernel(tc, xT, wgt, wk_words, wk_scales, wv, bg, res, offs, o
             nt0, count, j0, width = UNITS[u]
             if a == 0:
                 ke_banks[u] = bank([P, count, width], KE_BANK[u])
-            x_codes, x_scales = xq[a]
+            x_codes, x_scales = xq[a, j0 // JH]
+            j0 = j0 % JH
             step = JH if width == JH else P
             for c in range(count):
                 nt = nt0 + c
@@ -204,7 +203,8 @@ def tile_list_hway_kernel(tc, xT, wgt, wk_words, wk_scales, wv, bg, res, offs, o
             nt0, count, j0, width = UNITS[u]
             if a == 0:
                 ve_banks[u] = bank([P, count, width], VE_BANK[u])
-            x_codes, x_scales = xq[a]
+            x_codes, x_scales = xq[a, j0 // JH]
+            j0 = j0 % JH
             for c in range(count):
                 v_codes, v_scales = vq[a, nt0 + c]
                 nc.tensor.matmul_mx(
@@ -217,7 +217,7 @@ def tile_list_hway_kernel(tc, xT, wgt, wk_words, wk_scales, wv, bg, res, offs, o
         rests = {}
 
         def gate_on_vector(u, tag):
-            product = keep.tile([P, 1, JH], F32, name="product%d" % u, tag=tag, align_bytes=64)
+            product = keep.tile([P, UNITS[u][1], UNITS[u][3]], F32, name="product%d" % u, tag=tag, align_bytes=64)
             nc.vector.tensor_tensor(product[:], diffs[u][:], rests[u][:], ALU.mult)
             diffs[u] = product
 
@@ -242,57 +242,6 @@ def tile_list_hway_kernel(tc, xT, wgt, wk_words, wk_scales, wv, bg, res, offs, o
                 nc.vector.tensor_tensor(result[:, :, cols], ve_banks[u][:, :, cols], diffs[u][:, :, cols], ALU.subtract)
                 nc.sync.dma_start(unit_of(out, u)[:, :, cols], result[:, :, cols])
 
-        blocks = JH // P
-        res_turned = {}
-        gate_turned = {}
-        diff_turned = {}
-
-        def turn(source):
-            turned = bank([P, blocks, P], TURN_BANK)
-            for b in range(blocks):
-                nc.tensor.transpose(turned[:, b, :], source[:, b * P:(b + 1) * P], identity[:])
-            return turned
-
-        def turn_res(u):
-            res_turned[u] = keep.tile([P, blocks, P], F32, name="res_turned%d" % u)
-            nc.scalar.copy(res_turned[u][:], turn(res_sb[u][:, 0, :])[:])
-
-        def turned_value_sum(u):
-            nt, count, j0, width = UNITS[u]
-            ve_banks[u] = bank([P, blocks, P], VE_BANK[u])
-            for b in range(blocks):
-                cols = slice(j0 + b * P, j0 + (b + 1) * P)
-                for a in range(PASSES):
-                    x_codes, x_scales = xq[a]
-                    v_codes, v_scales = vq[a, nt]
-                    nc.tensor.matmul_mx(
-                        ve_banks[u][:, b, :], lhsT=x_codes[:, cols].bitcast(FP8X4), lhsT_scale=x_scales[:, cols],
-                        rhs=v_codes.bitcast(FP8X4), rhs_scale=v_scales, start=(a == 0), stop=(a == PASSES - 1))
-
-        def open_turned(u):
-            nt = UNITS[u][0]
-            gate = keep.tile([P, JH], F32, name="gate%d" % u)
-            nc.scalar.activation(gate[:], ke_banks[u][:, 0, :], ACT.Sigmoid, bias=bias[:, nt:nt + 1])
-            gate_turned[u] = turn(gate[:])
-            diff_turned[u] = keep.tile([P, blocks, P], F32, name="diff_turned%d" % u, tag="diff_turned", align_bytes=64)
-            nc.vector.tensor_tensor(diff_turned[u][:], ve_banks[u][:], res_turned[u][:], ALU.subtract)
-
-        def gate_turned_unit(u):
-            gated = keep.tile([P, blocks, P], F32, name="gated%d" % u)
-            nc.vector.tensor_tensor(gated[:], gate_turned[u][:], diff_turned[u][:], ALU.mult)
-            diff_turned[u] = gated
-
-        def close_turned(u):
-            total = bank([P, blocks, P], VE_BANK[u])
-            for b in range(blocks):
-                nc.tensor.matmul(total[:, b, :], res_turned[u][:, b, :], identity[:], start=True, stop=False,
-                                 is_transpose=True)
-                nc.tensor.matmul(total[:, b, :], diff_turned[u][:, b, :], identity[:], start=False, stop=True,
-                                 is_transpose=True)
-            result = keep.tile([P, blocks, P], F32, name="result%d" % u)
-            nc.scalar.copy(result[:], total[:])
-            nc.sync.dma_start(unit_of(out, u)[:, 0, :], result[:].rearrange("p b j -> p (b j)"))
-
         def gate_sums(u):
             for a in range(PASSES):
                 gate_sum(u, a)
@@ -309,20 +258,20 @@ def tile_list_hway_kernel(tc, xT, wgt, wk_words, wk_scales, wv, bg, res, offs, o
                     lay_pair(early[h][:], 0, i - 1, h * JH, JH)
         gather(1, 0, 0, J)
         gather(1, 1, 0, J)
-        xq[0] = mx_operand("xg0", J, "plane1_1")
-        for h in range(2):
-            make_xq(early[h][:], 0, h * JH, JH)
+        xq[0, 0] = mx_operand("xg0_0", JH, "plane1_1")
+        make_xq(early[0][:], 0, 0, JH)
         gather(1, 2, 0, J)
         round_wv(0, 2, [0])
         make_vq(0, 2, [0], "plane1_2")
-        for u in range(4):
+        for u in range(2):
             gate_sum(u, 0)
-        for u in range(4):
+        for u in range(2):
             value_sum(u, 0)
         late = keep.tile([P, J, PACK], BF16, name="late", tag="wv_raw0_0", align_bytes=64)
         lay_pair(late[:], 1, 0, 0, J)
         round_wv(0, 2, [1])
-        xq[1] = mx_operand("xg1", J, "xg1")
+        for h in range(2):
+            xq[1, h] = mx_operand("xg1_%d" % h, JH, "xg1_%d" % h)
 
         gather(1, PACK - 1, 0, JQ)
         gather(1, PACK - 1, JQ, JQ)
@@ -333,36 +282,29 @@ def tile_list_hway_kernel(tc, xT, wgt, wk_words, wk_scales, wv, bg, res, offs, o
             make_xq(piece, 1, q * JQ, JQ)
             if q == 0:
                 make_vq(0, 2, [1], "plane1_3")
-            gate_sum(q, 1)
-            value_sum(q, 1)
-        open_unit(0)
+            if q == 1:
+                xq[0, 1] = mx_operand("xg0_1", JH, "wv_bf0_1")
+                make_xq(early[1][:], 0, JH, JH)
+            if q < 2:
+                gate_sum(q, 1)
+                value_sum(q, 1)
+            else:
+                gate_sums(q)
+                value_sums(q)
+        open_unit(0, False)
+        gate_on_vector(0, "product0")
         open_unit(1)
-        open_unit(2)
-        round_wv(2, 1, [0, 1])
-        close_unit(0, 1, "res1")
-        make_vq(2, 1, [0, 1], "wv2")
-        gate_sums(4)
-        value_sums(4)
-        open_unit(3)
-        gate_sums(5)
-        value_sums(5)
-        round_wv(3, 1, [0, 1])
-        close_unit(1, 1, "res2")
-        make_vq(3, 1, [0, 1], "wv3")
-        open_unit(4)
-        gate_sums(6)
-        turn_res(6)
-        turned_value_sum(6)
-        close_unit(2, 1, "res3")
-        open_turned(6)
-        value_sums(7)
-        open_unit(5, False)
-        gate_sums(7)
-        close_unit(3, 1, "res4")
-        open_unit(7)
-        gate_turned_unit(6)
-        gate_on_vector(5, "res7")
-        close_turned(6)
-        close_unit(4, 1, "res5")
-        close_unit(5, 1, "result5")
-        close_unit(7, 2, "result7")
+        last = len(UNITS) - 1
+        for u in range(2, len(UNITS)):
+            open_unit(u, u != last - 1)
+            if u == last:
+                gate_on_vector(last - 1, "res7")
+            close_unit(u - 2, 1, "res%d" % (u - 1))
+            if u in (2, 4):
+                round_wv(u // 2 + 1, 1, [0, 1])
+                make_vq(u // 2 + 1, 1, [0, 1], "wv%d" % u)
+            if 4 <= u + 2 <= last:
+                gate_sums(u + 2)
+                value_sums(u + 2)
+        close_unit(last - 1, 1, "result6")
+        close_unit(last, 2, "result7")

@@ -296,15 +296,15 @@ def tile_list_hway_kernel(tc, xT, wgt, wk_words, wk_scales, wv, bg, res, offs, o
         open_unit(1)
         last = len(UNITS) - 1
         for u in range(2, len(UNITS)):
-            open_unit(u, u != last - 1)
+            open_unit(u, u != last)
             if u == last:
-                gate_on_vector(last - 1, "res7")
-            close_unit(u - 2, 1, "res%d" % (u - 1))
+                gate_on_vector(last, "product7")
+            close_unit(u - 2, 1, "result%d" % (u - 2))
             if u in (2, 4):
                 round_wv(u // 2 + 1, 1, [0, 1])
                 make_vq(u // 2 + 1, 1, [0, 1], "wv%d" % u)
             if 4 <= u + 2 <= last:
                 gate_sums(u + 2)
                 value_sums(u + 2)
-        close_unit(last - 1, 1, "result6")
-        close_unit(last, 2, "result7")
+        close_unit(last, 1, "result7")
+        close_unit(last - 1, 2, "result6")

@@ -23,38 +23,36 @@ P = 128
 QUAD = 32
 GROUP = 16
 PACK = 4
+RUN = 4
+SCALE_ROWS = 4
 K_PASS = P * PACK
 PASSES = K // K_PASS
 JH = 512
 JQ = 256
 NH = 256
 N_TILES = N // P
-KE_BANK = [0, 1, 2, 7, 0, 2, 7, 0]
-VE_BANK = [3, 4, 5, 6, 1, 3, 4, 5]
 
-UNITS = [(0, 2, q * JQ, JQ) for q in range(4)] + [(nt, 1, h * JH, JH) for nt in (2, 3) for h in range(2)]
+UNITS = [(0, 2, q * JQ, JQ) for q in range(J // JQ)] + [(nt, 1, h * JH, JH) for nt in (2, 3) for h in range(2)]
+KE_BANKS, VE_BANKS = 3, 5
 
 
 def tile_list_hway_kernel(tc, xT, wgt, wk_words, wk_scales, wv, bg, res, offs, out):
     nc = tc.nc
     with ExitStack() as ctx:
         keep = ctx.enter_context(tc.tile_pool(name="keep", bufs=1))
-        work = ctx.enter_context(tc.tile_pool(name="work", bufs=4))
-        psum = ctx.enter_context(tc.psum_pool(name="psum", bufs=1))
-
-        def bank(shape, number):
-            return psum.tile(shape, F32, name="bank%d" % number)
+        work = ctx.enter_context(tc.tile_pool(name="work", bufs=J // JQ))
+        ke_pool = ctx.enter_context(tc.psum_pool(name="ke_pool", bufs=KE_BANKS))
+        ve_pool = ctx.enter_context(tc.psum_pool(name="ve_pool", bufs=VE_BANKS))
 
         offsets = keep.tile([P, J // GROUP], U16, name="offsets")
         weights = keep.tile([P, J], F32, name="weights", align_bytes=64)
-        planes = [[keep.tile([P, T], F32, name="plane%d_%d" % (a, i), tag="plane%d_%d" % (a, i), align_bytes=64)
-                   for i in range(PACK)] for a in range(PASSES)]
+        planes = [[keep.tile([P, T], F32, name="plane%d_%d" % (a, i), align_bytes=64) for i in range(PACK)]
+                  for a in range(PASSES)]
         wk_codes = [keep.tile([P, 2 * N], U8, name="wk_codes%d" % a, align_bytes=64) for a in range(PASSES)]
         wk_scale_rows = keep.tile([P, PASSES, N], U8, name="wk_scale_rows", align_bytes=64)
-        wv_raw = [[keep.tile([P, PACK, NH], F32, name="wv_raw%d_%d" % (a, m), tag="wv_raw%d_%d" % (a, m), align_bytes=64)
-                   for m in range(2)] for a in range(PASSES)]
-        res_sb = [keep.tile([P, unit[1], unit[3]], F32, name="res%d" % u, tag="res%d" % u, align_bytes=64)
-                  for u, unit in enumerate(UNITS)]
+        wv_first = [keep.tile([P, PACK, NH], F32, name="wv_first%d" % a, align_bytes=64) for a in range(PASSES)]
+        wv_second = keep.tile([P, PASSES, PACK, NH], F32, name="wv_second")
+        res_sb = [keep.tile([P, unit[1], unit[3]], F32, name="res%d" % u) for u, unit in enumerate(UNITS)]
 
         bias_rows = keep.tile([P, P], F32, name="bias_rows")
         identity = keep.tile([P, P], F32, name="identity")
@@ -63,13 +61,17 @@ def tile_list_hway_kernel(tc, xT, wgt, wk_words, wk_scales, wv, bg, res, offs, o
         nc.scalar.activation(bias_rows[:], bias_rows[:], ACT.Sigmoid)
         nc.vector.memset(wk_scale_rows[:].rearrange("p a n -> p (a n)").bitcast(I32), 0)
 
-        def load_plane(a, i):
-            rows = xT[a * K_PASS:(a + 1) * K_PASS, :].rearrange("(p i) t -> p i t", i=PACK)
-            nc.sync.dma_start(planes[a][i][:], rows[:, i, :])
+        def rows_of_pass(matrix, a):
+            return matrix[a * K_PASS:(a + 1) * K_PASS, :].rearrange("(p i) c -> p i c", i=PACK)
 
-        def load_wv(a, m):
-            rows = wv[a * K_PASS:(a + 1) * K_PASS, :].rearrange("(p i) n -> p i n", i=PACK)
-            nc.sync.dma_start(wv_raw[a][m][:], rows[:, :, m * NH:(m + 1) * NH])
+        def load_plane(a, i):
+            nc.sync.dma_start(planes[a][i][:], rows_of_pass(xT, a)[:, i, :])
+
+        def load_wv_first(a):
+            nc.sync.dma_start(wv_first[a][:], rows_of_pass(wv, a)[:, :, :NH])
+
+        def load_wv_second(a):
+            nc.sync.dma_start(wv_second[:, a, :, :], rows_of_pass(wv, a)[:, :, NH:])
 
         def load_wk(a):
             nc.sync.dma_start(wk_codes[a][:].bitcast(I32), wk_words[a].bitcast(I32))
@@ -106,27 +108,27 @@ def tile_list_hway_kernel(tc, xT, wgt, wk_words, wk_scales, wv, bg, res, offs, o
             load_plane(0, i)
         for q in range(P // QUAD):
             nc.sync.dma_start(
-                wk_scale_rows[QUAD * q:QUAD * q + 4, :, :].bitcast(I32),
-                wk_scales[:, 4 * q:4 * q + 4, :].rearrange("a r n -> r a n").bitcast(I32),
+                wk_scale_rows[QUAD * q:QUAD * q + SCALE_ROWS, :, :].bitcast(I32),
+                wk_scales[:, SCALE_ROWS * q:SCALE_ROWS * (q + 1), :].rearrange("a r n -> r a n").bitcast(I32),
             )
         nc.sync.dma_start(bias_rows[0:N_TILES, :], bg.rearrange("(c p) -> c p", p=P))
         load_plane(1, 0)
         load_plane(1, 1)
         load_wk(0)
-        load_wv(0, 0)
+        load_wv_first(0)
         load_plane(1, 2)
-        load_wv(1, 0)
+        load_wv_first(1)
         load_plane(1, 3)
         load_wk(1)
         load_res(0)
         load_res(1)
-        load_wv(0, 1)
-        load_wv(1, 1)
+        load_wv_second(0)
+        load_wv_second(1)
         for u in range(2, len(UNITS)):
             load_res(u)
 
         minus_bias = keep.tile([P, N_TILES], F32, name="minus_bias")
-        bias_turned = bank([P, P], 0)
+        bias_turned = ke_pool.tile([P, P], F32, name="ke")
         nc.tensor.transpose(bias_turned[:], bias_rows[:], identity[:])
         nc.scalar.mul(minus_bias[:], bias_turned[:, 0:N_TILES], -1.0)
 
@@ -147,51 +149,51 @@ def tile_list_hway_kernel(tc, xT, wgt, wk_words, wk_scales, wv, bg, res, offs, o
                 ALU.mult,
             )
 
-        def lay_pair(rounded, a, i0, j0, width):
+        def round_pair(rounded, a, i0, j0, width):
             nc.scalar.copy(rounded[:, :, i0:i0 + 2], picked[a][:, i0:i0 + 2, j0:j0 + width].rearrange("p i w -> p w i"))
 
-        def make_xq(rounded, a, j0, width):
+        def quantise_xg(rounded, a, j0, width):
             codes, scales = xq[a, j0 // JH]
             c0 = j0 % JH
             nc.vector.quantize_mx(codes[:, c0:c0 + width].bitcast(FP8X4), scales[:, c0:c0 + width],
                                   rounded.rearrange("p w i -> p (w i)"))
 
-        wv_bf = {}
+        def round_wv_first(a):
+            rounded = keep.tile([P, NH, PACK], BF16, name="wv_first_bf%d" % a, align_bytes=64)
+            nc.scalar.copy(rounded[:].rearrange("p (c r) i -> p c i r", r=RUN),
+                           wv_first[a][:].rearrange("p i (c r) -> p c i r", r=RUN))
+            return rounded
 
-        def round_wv(nt0, count, passes):
-            width = count * P
-            c0 = (nt0 % 2) * P
-            grouped = keep.tile([P, len(passes), width, PACK], BF16, name="wv_bf%d_%d" % (nt0, passes[0]), tag="wv_bf%d_%d" % (nt0, passes[0]),
-                                align_bytes=64)
-            wv_bf[nt0, passes[0]] = grouped
-            for place, a in enumerate(passes):
-                nc.scalar.copy(grouped[:, place, :, :].rearrange("p (c r) i -> p c i r", r=4),
-                               wv_raw[a][nt0 // 2][:, :, c0:c0 + width].rearrange("p i (c r) -> p c i r", r=4))
+        def quantise_wv_first(rounded, a, tag):
+            codes, scales = mx_operand("wv_first%d" % a, NH, tag)
+            nc.vector.quantize_mx(codes.bitcast(FP8X4), scales, rounded[:].rearrange("p n i -> p (n i)"))
+            for nt in range(NH // P):
+                vq[a, nt] = (codes[:, nt * P:(nt + 1) * P], scales[:, nt * P:(nt + 1) * P])
 
-        def make_vq(nt0, count, passes, tag):
-            width = count * P
-            codes, scales = mx_operand("wv%d_%d" % (nt0, passes[0]), len(passes) * width, tag)
-            nc.vector.quantize_mx(codes.bitcast(FP8X4), scales,
-                                  wv_bf[nt0, passes[0]][:].rearrange("p a w i -> p (a w i)"))
-            for place, a in enumerate(passes):
-                for c in range(count):
-                    cols = slice(place * width + c * P, place * width + (c + 1) * P)
-                    vq[a, nt0 + c] = (codes[:, cols], scales[:, cols])
+        def make_wv_second(nt):
+            c0 = nt * P - NH
+            rounded = keep.tile([P, PASSES, P, PACK], BF16, name="wv_second_bf%d" % nt, align_bytes=64)
+            nc.scalar.copy(rounded[:].rearrange("p a (c r) i -> p a c i r", r=RUN),
+                           wv_second[:, :, :, c0:c0 + P].rearrange("p a i (c r) -> p a c i r", r=RUN))
+            codes, scales = mx_operand("wv_second%d" % nt, PASSES * P, "wv_second%d_codes" % nt)
+            nc.vector.quantize_mx(codes.bitcast(FP8X4), scales, rounded[:].rearrange("p a n i -> p (a n i)"))
+            for a in range(PASSES):
+                vq[a, nt] = (codes[:, a * P:(a + 1) * P], scales[:, a * P:(a + 1) * P])
 
         ke_banks = {}
         ve_banks = {}
 
-        def gate_sum(u, a):
+        def ke_pass(u, a):
             nt0, count, j0, width = UNITS[u]
             if a == 0:
-                ke_banks[u] = bank([P, count, width], KE_BANK[u])
+                ke_banks[u] = ke_pool.tile([P, count, width], F32, name="ke")
             x_codes, x_scales = xq[a, j0 // JH]
-            j0 = j0 % JH
+            c0 = j0 % JH
             step = JH if width == JH else P
             for c in range(count):
                 nt = nt0 + c
                 for b in range(0, width, step):
-                    cols = slice(j0 + b, j0 + b + step)
+                    cols = slice(c0 + b, c0 + b + step)
                     nc.tensor.matmul_mx(
                         ke_banks[u][:, c, b:b + step], lhsT=wk_codes[a][:, 2 * P * nt:2 * P * (nt + 1)].bitcast(FP4X4),
                         lhsT_scale=wk_scale_rows[:, a, P * nt:P * (nt + 1)],
@@ -199,112 +201,96 @@ def tile_list_hway_kernel(tc, xT, wgt, wk_words, wk_scales, wv, bg, res, offs, o
                         start=(a == 0 and c == 0 and b == 0),
                         stop=(a == PASSES - 1 and c == count - 1 and b + step == width))
 
-        def value_sum(u, a):
+        def ve_pass(u, a):
             nt0, count, j0, width = UNITS[u]
             if a == 0:
-                ve_banks[u] = bank([P, count, width], VE_BANK[u])
+                ve_banks[u] = ve_pool.tile([P, count, width], F32, name="ve")
             x_codes, x_scales = xq[a, j0 // JH]
-            j0 = j0 % JH
+            cols = slice(j0 % JH, j0 % JH + width)
             for c in range(count):
                 v_codes, v_scales = vq[a, nt0 + c]
                 nc.tensor.matmul_mx(
                     ve_banks[u][:, c, :], lhsT=v_codes.bitcast(FP8X4), lhsT_scale=v_scales,
-                    rhs=x_codes[:, j0:j0 + width].bitcast(FP8X4), rhs_scale=x_scales[:, j0:j0 + width],
+                    rhs=x_codes[:, cols].bitcast(FP8X4), rhs_scale=x_scales[:, cols],
                     start=(a == 0 and c == 0), stop=(a == PASSES - 1 and c == count - 1))
 
-        diffs = {}
+        def all_passes(u):
+            for a in range(PASSES):
+                ke_pass(u, a)
+            for a in range(PASSES):
+                ve_pass(u, a)
 
-        rests = {}
+        gated = {}
 
-        def gate_on_vector(u, tag):
-            product = keep.tile([P, UNITS[u][1], UNITS[u][3]], F32, name="product%d" % u, tag=tag, align_bytes=64)
-            nc.vector.tensor_tensor(product[:], diffs[u][:], rests[u][:], ALU.mult)
-            diffs[u] = product
-
-        def open_unit(u, on_gpsimd=True):
+        def open_unit(u, engine):
             nt0, count, j0, width = UNITS[u]
             rest = work.tile([P, count, width], F32, name="rest")
-            diffs[u] = work.tile([P, count, width], F32, name="diff")
+            gated[u] = work.tile([P, count, width], F32, name="gated")
             for c in range(count):
                 nc.scalar.activation(rest[:, c, :], ke_banks[u][:, c, :], ACT.Sigmoid,
                                      bias=minus_bias[:, nt0 + c:nt0 + c + 1], scale=-1.0)
-            nc.vector.tensor_tensor(diffs[u][:], ve_banks[u][:], res_sb[u][:], ALU.subtract)
-            rests[u] = rest
-            if on_gpsimd:
-                nc.gpsimd.tensor_tensor(diffs[u][:], diffs[u][:], rest[:], ALU.mult)
+            nc.vector.tensor_tensor(gated[u][:], ve_banks[u][:], res_sb[u][:], ALU.subtract)
+            engine.tensor_tensor(gated[u][:], gated[u][:], rest[:], ALU.mult)
 
-        def close_unit(u, pieces, tag):
+        def close_unit(u, pieces):
             nt0, count, j0, width = UNITS[u]
-            result = keep.tile([P, count, width], F32, name="result%d" % u, tag=tag, align_bytes=64)
             step = width // pieces
             for c0 in range(0, width, step):
                 cols = slice(c0, c0 + step)
-                nc.vector.tensor_tensor(result[:, :, cols], ve_banks[u][:, :, cols], diffs[u][:, :, cols], ALU.subtract)
-                nc.sync.dma_start(unit_of(out, u)[:, :, cols], result[:, :, cols])
+                result = keep.tile([P, count, step], F32, name="result%d_%d" % (u, c0))
+                nc.vector.tensor_tensor(result[:], ve_banks[u][:, :, cols], gated[u][:, :, cols], ALU.subtract)
+                nc.sync.dma_start(unit_of(out, u)[:, :, cols], result[:])
 
-        def gate_sums(u):
-            for a in range(PASSES):
-                gate_sum(u, a)
-
-        def value_sums(u):
-            for a in range(PASSES):
-                value_sum(u, a)
-
-        early = [keep.tile([P, JH, PACK], BF16, name="early%d" % h, align_bytes=64) for h in range(2)]
+        rounded0 = [keep.tile([P, JH, PACK], BF16, name="rounded0_%d" % h, align_bytes=64) for h in range(2)]
         for i in range(PACK):
             gather(0, i, 0, J)
             if i % 2 == 1:
                 for h in range(2):
-                    lay_pair(early[h][:], 0, i - 1, h * JH, JH)
+                    round_pair(rounded0[h][:], 0, i - 1, h * JH, JH)
         gather(1, 0, 0, J)
         gather(1, 1, 0, J)
         xq[0, 0] = mx_operand("xg0_0", JH, "plane1_1")
-        make_xq(early[0][:], 0, 0, JH)
+        quantise_xg(rounded0[0][:], 0, 0, JH)
         gather(1, 2, 0, J)
-        round_wv(0, 2, [0])
-        make_vq(0, 2, [0], "plane1_2")
+        quantise_wv_first(round_wv_first(0), 0, "wv_first0_codes")
         for u in range(2):
-            gate_sum(u, 0)
+            ke_pass(u, 0)
         for u in range(2):
-            value_sum(u, 0)
-        late = keep.tile([P, J, PACK], BF16, name="late", tag="wv_raw0_0", align_bytes=64)
-        lay_pair(late[:], 1, 0, 0, J)
-        round_wv(0, 2, [1])
+            ve_pass(u, 0)
+        rounded1 = keep.tile([P, J, PACK], BF16, name="rounded1", tag="wv_first0", align_bytes=64)
+        round_pair(rounded1[:], 1, 0, 0, J)
+        wv_first1_bf = round_wv_first(1)
         for h in range(2):
-            xq[1, h] = mx_operand("xg1_%d" % h, JH, "xg1_%d" % h)
+            xq[1, h] = mx_operand("xg1_%d" % h, JH, "xg1_%d_codes" % h)
 
         gather(1, PACK - 1, 0, JQ)
         gather(1, PACK - 1, JQ, JQ)
         gather(1, PACK - 1, JH, JH)
-        for q in range(4):
-            piece = late[:, q * JQ:(q + 1) * JQ, :]
-            lay_pair(piece, 1, 2, q * JQ, JQ)
-            make_xq(piece, 1, q * JQ, JQ)
+        for q in range(J // JQ):
+            piece = rounded1[:, q * JQ:(q + 1) * JQ, :]
+            round_pair(piece, 1, 2, q * JQ, JQ)
+            quantise_xg(piece, 1, q * JQ, JQ)
             if q == 0:
-                make_vq(0, 2, [1], "plane1_3")
+                quantise_wv_first(wv_first1_bf, 1, "plane1_3")
             if q == 1:
-                xq[0, 1] = mx_operand("xg0_1", JH, "wv_bf0_1")
-                make_xq(early[1][:], 0, JH, JH)
-            if q < 2:
-                gate_sum(q, 1)
-                value_sum(q, 1)
+                xq[0, 1] = mx_operand("xg0_1", JH, "wv_first_bf1")
+                quantise_xg(rounded0[1][:], 0, JH, JH)
+            if q * JQ < JH:
+                ke_pass(q, 1)
+                ve_pass(q, 1)
             else:
-                gate_sums(q)
-                value_sums(q)
-        open_unit(0, False)
-        gate_on_vector(0, "product0")
-        open_unit(1)
+                all_passes(q)
+
         last = len(UNITS) - 1
+        open_unit(0, nc.vector)
+        open_unit(1, nc.gpsimd)
         for u in range(2, len(UNITS)):
-            open_unit(u, u != last)
-            if u == last:
-                gate_on_vector(last, "product7")
-            close_unit(u - 2, 1, "result%d" % (u - 2))
-            if u in (2, 4):
-                round_wv(u // 2 + 1, 1, [0, 1])
-                make_vq(u // 2 + 1, 1, [0, 1], "wv%d" % u)
-            if 4 <= u + 2 <= last:
-                gate_sums(u + 2)
-                value_sums(u + 2)
-        close_unit(last, 1, "result7")
-        close_unit(last - 1, 2, "result6")
+            open_unit(u, nc.vector if u == last else nc.gpsimd)
+            close_unit(u - 2, 1)
+            if u + 2 <= last:
+                nt = UNITS[u + 2][0]
+                if (0, nt) not in vq:
+                    make_wv_second(nt)
+                all_passes(u + 2)
+        close_unit(last, 1)
+        close_unit(last - 1, 2)

@@ -33,7 +33,8 @@ NH = 256
 N_TILES = N // P
 
 UNITS = [(0, 2, q * JQ, JQ) for q in range(J // JQ)] + [(nt, 1, h * JH, JH) for nt in (2, 3) for h in range(2)]
-KE_BANKS, VE_BANKS = 3, 5
+KE_BANK = [0, 1, 2, 7, 0, 2, 7, 0]
+VE_BANK = [3, 4, 5, 6, 1, 3, 4, 5]
 
 
 def tile_list_hway_kernel(tc, xT, wgt, wk_words, wk_scales, wv, bg, res, offs, out):
@@ -41,8 +42,10 @@ def tile_list_hway_kernel(tc, xT, wgt, wk_words, wk_scales, wv, bg, res, offs, o
     with ExitStack() as ctx:
         keep = ctx.enter_context(tc.tile_pool(name="keep", bufs=1))
         work = ctx.enter_context(tc.tile_pool(name="work", bufs=J // JQ))
-        ke_pool = ctx.enter_context(tc.psum_pool(name="ke_pool", bufs=KE_BANKS))
-        ve_pool = ctx.enter_context(tc.psum_pool(name="ve_pool", bufs=VE_BANKS))
+        psum = ctx.enter_context(tc.psum_pool(name="psum", bufs=1))
+
+        def bank(shape, number):
+            return psum.tile(shape, F32, name="bank%d" % number)
 
         offsets = keep.tile([P, J // GROUP], U16, name="offsets")
         weights = keep.tile([P, J], F32, name="weights", align_bytes=64)
@@ -51,7 +54,7 @@ def tile_list_hway_kernel(tc, xT, wgt, wk_words, wk_scales, wv, bg, res, offs, o
         wk_codes = [keep.tile([P, 2 * N], U8, name="wk_codes%d" % a, align_bytes=64) for a in range(PASSES)]
         wk_scale_rows = keep.tile([P, PASSES, N], U8, name="wk_scale_rows", align_bytes=64)
         wv_first = [keep.tile([P, PACK, NH], F32, name="wv_first%d" % a, align_bytes=64) for a in range(PASSES)]
-        wv_second = keep.tile([P, PASSES, PACK, NH], F32, name="wv_second")
+        wv_second = [keep.tile([P, PACK, NH], F32, name="wv_second%d" % a, align_bytes=64) for a in range(PASSES)]
         res_sb = [keep.tile([P, unit[1], unit[3]], F32, name="res%d" % u) for u, unit in enumerate(UNITS)]
 
         bias_rows = keep.tile([P, P], F32, name="bias_rows")
@@ -71,7 +74,7 @@ def tile_list_hway_kernel(tc, xT, wgt, wk_words, wk_scales, wv, bg, res, offs, o
             nc.sync.dma_start(wv_first[a][:], rows_of_pass(wv, a)[:, :, :NH])
 
         def load_wv_second(a):
-            nc.sync.dma_start(wv_second[:, a, :, :], rows_of_pass(wv, a)[:, :, NH:])
+            nc.sync.dma_start(wv_second[a][:], rows_of_pass(wv, a)[:, :, NH:])
 
         def load_wk(a):
             nc.sync.dma_start(wk_codes[a][:].bitcast(I32), wk_words[a].bitcast(I32))
@@ -128,7 +131,7 @@ def tile_list_hway_kernel(tc, xT, wgt, wk_words, wk_scales, wv, bg, res, offs, o
             load_res(u)
 
         minus_bias = keep.tile([P, N_TILES], F32, name="minus_bias")
-        bias_turned = ke_pool.tile([P, P], F32, name="ke")
+        bias_turned = bank([P, P], KE_BANK[0])
         nc.tensor.transpose(bias_turned[:], bias_rows[:], identity[:])
         nc.scalar.mul(minus_bias[:], bias_turned[:, 0:N_TILES], -1.0)
 
@@ -158,10 +161,12 @@ def tile_list_hway_kernel(tc, xT, wgt, wk_words, wk_scales, wv, bg, res, offs, o
             nc.vector.quantize_mx(codes[:, c0:c0 + width].bitcast(FP8X4), scales[:, c0:c0 + width],
                                   rounded.rearrange("p w i -> p (w i)"))
 
+        def round_wv(rounded, rows):
+            nc.scalar.copy(rounded.rearrange("p (c r) i -> p c i r", r=RUN), rows.rearrange("p i (c r) -> p c i r", r=RUN))
+
         def round_wv_first(a):
             rounded = keep.tile([P, NH, PACK], BF16, name="wv_first_bf%d" % a, align_bytes=64)
-            nc.scalar.copy(rounded[:].rearrange("p (c r) i -> p c i r", r=RUN),
-                           wv_first[a][:].rearrange("p i (c r) -> p c i r", r=RUN))
+            round_wv(rounded[:], wv_first[a][:])
             return rounded
 
         def quantise_wv_first(rounded, a, tag):
@@ -173,8 +178,8 @@ def tile_list_hway_kernel(tc, xT, wgt, wk_words, wk_scales, wv, bg, res, offs, o
         def make_wv_second(nt):
             c0 = nt * P - NH
             rounded = keep.tile([P, PASSES, P, PACK], BF16, name="wv_second_bf%d" % nt, align_bytes=64)
-            nc.scalar.copy(rounded[:].rearrange("p a (c r) i -> p a c i r", r=RUN),
-                           wv_second[:, :, :, c0:c0 + P].rearrange("p a i (c r) -> p a c i r", r=RUN))
+            for a in range(PASSES):
+                round_wv(rounded[:, a, :, :], wv_second[a][:, :, c0:c0 + P])
             codes, scales = mx_operand("wv_second%d" % nt, PASSES * P, "wv_second%d_codes" % nt)
             nc.vector.quantize_mx(codes.bitcast(FP8X4), scales, rounded[:].rearrange("p a n i -> p (a n i)"))
             for a in range(PASSES):
@@ -186,7 +191,7 @@ def tile_list_hway_kernel(tc, xT, wgt, wk_words, wk_scales, wv, bg, res, offs, o
         def ke_pass(u, a):
             nt0, count, j0, width = UNITS[u]
             if a == 0:
-                ke_banks[u] = ke_pool.tile([P, count, width], F32, name="ke")
+                ke_banks[u] = bank([P, count, width], KE_BANK[u])
             x_codes, x_scales = xq[a, j0 // JH]
             c0 = j0 % JH
             step = JH if width == JH else P
@@ -204,7 +209,7 @@ def tile_list_hway_kernel(tc, xT, wgt, wk_words, wk_scales, wv, bg, res, offs, o
         def ve_pass(u, a):
             nt0, count, j0, width = UNITS[u]
             if a == 0:
-                ve_banks[u] = ve_pool.tile([P, count, width], F32, name="ve")
+                ve_banks[u] = bank([P, count, width], VE_BANK[u])
             x_codes, x_scales = xq[a, j0 // JH]
             cols = slice(j0 % JH, j0 % JH + width)
             for c in range(count):
@@ -249,10 +254,10 @@ def tile_list_hway_kernel(tc, xT, wgt, wk_words, wk_scales, wv, bg, res, offs, o
                     round_pair(rounded0[h][:], 0, i - 1, h * JH, JH)
         gather(1, 0, 0, J)
         gather(1, 1, 0, J)
-        xq[0, 0] = mx_operand("xg0_0", JH, "plane1_1")
-        quantise_xg(rounded0[0][:], 0, 0, JH)
-        gather(1, 2, 0, J)
         quantise_wv_first(round_wv_first(0), 0, "wv_first0_codes")
+        gather(1, 2, 0, J)
+        xq[0, 0] = mx_operand("xg0_0", JH, "plane1_2")
+        quantise_xg(rounded0[0][:], 0, 0, JH)
         for u in range(2):
             ke_pass(u, 0)
         for u in range(2):

@@ -227,7 +227,7 @@ def tile_list_hway_kernel(tc, xT, wgt, wk_words, wk_scales, wv, bg, res, offs, o
 
         gated = {}
 
-        def open_unit(u, engine):
+        def open_unit(u, engines):
             nt0, count, j0, width = UNITS[u]
             rest = work.tile([P, count, width], F32, name="rest")
             gated[u] = work.tile([P, count, width], F32, name="gated")
@@ -235,16 +235,16 @@ def tile_list_hway_kernel(tc, xT, wgt, wk_words, wk_scales, wv, bg, res, offs, o
                 nc.scalar.activation(rest[:, c, :], ke_banks[u][:, c, :], ACT.Sigmoid,
                                      bias=minus_bias[:, nt0 + c:nt0 + c + 1], scale=-1.0)
             nc.vector.tensor_tensor(gated[u][:], ve_banks[u][:], res_sb[u][:], ALU.subtract)
-            engine.tensor_tensor(gated[u][:], gated[u][:], rest[:], ALU.mult)
+            step = width // len(engines)
+            for place, engine in enumerate(engines):
+                cols = slice(place * step, (place + 1) * step)
+                engine.tensor_tensor(gated[u][:, :, cols], gated[u][:, :, cols], rest[:, :, cols], ALU.mult)
 
-        def close_unit(u, pieces):
-            nt0, count, j0, width = UNITS[u]
-            step = width // pieces
-            for c0 in range(0, width, step):
-                cols = slice(c0, c0 + step)
-                result = keep.tile([P, count, step], F32, name="result%d_%d" % (u, c0))
-                nc.vector.tensor_tensor(result[:], ve_banks[u][:, :, cols], gated[u][:, :, cols], ALU.subtract)
-                nc.sync.dma_start(unit_of(out, u)[:, :, cols], result[:])
+        def close_unit(u, c0, width):
+            cols = slice(c0, c0 + width)
+            result = keep.tile([P, UNITS[u][1], width], F32, name="result%d_%d" % (u, c0))
+            nc.vector.tensor_tensor(result[:], ve_banks[u][:, :, cols], gated[u][:, :, cols], ALU.subtract)
+            nc.sync.dma_start(unit_of(out, u)[:, :, cols], result[:])
 
         rounded0 = [keep.tile([P, JH, PACK], BF16, name="rounded0_%d" % h, align_bytes=64) for h in range(2)]
         for i in range(PACK):
@@ -271,7 +271,8 @@ def tile_list_hway_kernel(tc, xT, wgt, wk_words, wk_scales, wv, bg, res, offs, o
         gather(1, PACK - 1, 0, JQ)
         gather(1, PACK - 1, JQ, JQ)
         gather(1, PACK - 1, JH, JH)
-        for q in range(J // JQ):
+
+        def finish_quarter(q):
             piece = rounded1[:, q * JQ:(q + 1) * JQ, :]
             round_pair(piece, 1, 2, q * JQ, JQ)
             quantise_xg(piece, 1, q * JQ, JQ)
@@ -286,16 +287,21 @@ def tile_list_hway_kernel(tc, xT, wgt, wk_words, wk_scales, wv, bg, res, offs, o
             else:
                 all_passes(q)
 
+        for q in range(J // JQ - 1):
+            finish_quarter(q)
+
         last = len(UNITS) - 1
-        open_unit(0, nc.vector)
-        open_unit(1, nc.gpsimd)
+        open_unit(0, [nc.vector])
+        open_unit(1, [nc.gpsimd])
+        finish_quarter(J // JQ - 1)
         for u in range(2, len(UNITS)):
-            open_unit(u, nc.vector if u == last else nc.gpsimd)
-            close_unit(u - 2, 1)
+            open_unit(u, [nc.vector, nc.gpsimd] if u == last else [nc.gpsimd])
+            close_unit(u - 2, 0, UNITS[u - 2][3])
             if u + 2 <= last:
                 nt = UNITS[u + 2][0]
                 if (0, nt) not in vq:
                     make_wv_second(nt)
                 all_passes(u + 2)
-        close_unit(last, 1)
-        close_unit(last - 1, 2)
+        close_unit(last, 0, JQ)
+        close_unit(last - 1, 0, JH)
+        close_unit(last, JQ, JQ)

@@ -87,25 +87,24 @@ def tile_list_hway_kernel(tc, xT, wgt, wk_words, wk_scales, wv, bg, res, offs, o
             nc.sync.dma_start(res_sb[u][:], unit_of(res, u))
 
         w_rows = keep.tile([P, 2, QUAD], F32, name="w_rows", align_bytes=64)
-        w_turned = keep.tile([P, 2, QUAD], F32, name="w_turned", align_bytes=64)
-        w_spread = keep.tile([P, J // QUAD, 2, GROUP], F32, name="w_spread", align_bytes=64)
-        for q in range(P // QUAD):
-            nc.sync.dma_start(w_rows[QUAD * q:QUAD * (q + 1), :, :],
-                              wgt[QUAD * q:QUAD * (q + 1):GROUP, :].rearrange("g (b s) -> b g s", s=QUAD))
+        w_turned = keep.tile([P, 2, 2, GROUP], F32, name="w_turned", align_bytes=64)
+        w_spread = keep.tile([P, GROUP, 2, 2, GROUP], F32, name="w_spread", align_bytes=64)
+        nc.sync.dma_start(w_rows[:].rearrange("p e s -> p (e s)"),
+                          wgt[0:P:GROUP, :].rearrange("h (b c) -> h b c", b=GROUP))
         load_plane(0, 0)
         nc.sync.dma_start(offsets[:], offs)
-        for g in range(2):
-            nc.vector.transpose(w_turned[:, g, :], w_rows[:, g, :])
-        half_blocks = JH // QUAD
+        for e in range(2):
+            nc.vector.transpose(w_turned[:, e, :, :].rearrange("p g b -> p (g b)"), w_rows[:, e, :])
+        half_blocks = GROUP // 2
         for h in range(2):
             b = slice(half_blocks * h, half_blocks * (h + 1))
             nc.vector.tensor_copy(
-                w_spread[:, b, :, :],
-                w_turned[:, :, b].rearrange("p g b -> p b g").unsqueeze(3).to_broadcast([P, half_blocks, 2, GROUP]))
+                w_spread[:, b, :, :, :],
+                w_turned[:, :, :, b].rearrange("p e g b -> p b e g").unsqueeze(4).to_broadcast([P, half_blocks, 2, 2, GROUP]))
         for h in range(2):
             b = slice(half_blocks * h, half_blocks * (h + 1))
             nc.vector.transpose(weights[:, h * JH:(h + 1) * JH],
-                                w_spread[:, b, :, :].rearrange("p b g r -> p (b g r)"))
+                                w_spread[:, b, :, :, :].rearrange("p b e g r -> p (b e g r)"))
 
         for i in range(1, PACK):
             load_plane(0, i)
@@ -194,7 +193,7 @@ def tile_list_hway_kernel(tc, xT, wgt, wk_words, wk_scales, wv, bg, res, offs, o
                 ke_banks[u] = bank([P, count, width], KE_BANK[u])
             x_codes, x_scales = xq[a, j0 // JH]
             c0 = j0 % JH
-            step = JH if width == JH else P
+            step = width
             for c in range(count):
                 nt = nt0 + c
                 for b in range(0, width, step):

@@ -51,7 +51,7 @@ def tile_list_hway_kernel(tc, xT, wgt, wk_words, wk_scales, wv, bg, res, offs, o
         weights = keep.tile([P, J], F32, name="weights", align_bytes=64)
         planes = [[keep.tile([P, T], F32, name="plane%d_%d" % (a, i), align_bytes=64) for i in range(PACK)]
                   for a in range(PASSES)]
-        wk_codes = [keep.tile([P, 2 * N], U8, name="wk_codes%d" % a, align_bytes=64) for a in range(PASSES)]
+        wk_codes = keep.tile([P, PASSES, 2 * N], U8, name="wk_codes", align_bytes=64)
         wk_scale_rows = keep.tile([P, PASSES, N], U8, name="wk_scale_rows", align_bytes=64)
         wv_first = [keep.tile([P, PACK, NH], F32, name="wv_first%d" % a, align_bytes=64) for a in range(PASSES)]
         wv_second = [keep.tile([P, PACK, NH], F32, name="wv_second%d" % a, align_bytes=64) for a in range(PASSES)]
@@ -75,9 +75,6 @@ def tile_list_hway_kernel(tc, xT, wgt, wk_words, wk_scales, wv, bg, res, offs, o
 
         def load_wv_second(a):
             nc.sync.dma_start(wv_second[a][:], rows_of_pass(wv, a)[:, :, NH:])
-
-        def load_wk(a):
-            nc.sync.dma_start(wk_codes[a][:].bitcast(I32), wk_words[a].bitcast(I32))
 
         def unit_of(matrix, u):
             nt0, count, j0, width = UNITS[u]
@@ -116,12 +113,11 @@ def tile_list_hway_kernel(tc, xT, wgt, wk_words, wk_scales, wv, bg, res, offs, o
         nc.sync.dma_start(bias_rows[0:N_TILES, :], bg.rearrange("(c p) -> c p", p=P))
         load_plane(1, 0)
         load_plane(1, 1)
-        load_wk(0)
         load_wv_first(0)
         load_plane(1, 2)
         load_wv_first(1)
         load_plane(1, 3)
-        load_wk(1)
+        nc.sync.dma_start(wk_codes[:].bitcast(I32), wk_words.rearrange("a p n -> p a n").bitcast(I32))
         load_res(0)
         load_res(1)
         load_wv_second(0)
@@ -199,7 +195,7 @@ def tile_list_hway_kernel(tc, xT, wgt, wk_words, wk_scales, wv, bg, res, offs, o
                 for b in range(0, width, step):
                     cols = slice(c0 + b, c0 + b + step)
                     nc.tensor.matmul_mx(
-                        ke_banks[u][:, c, b:b + step], lhsT=wk_codes[a][:, 2 * P * nt:2 * P * (nt + 1)].bitcast(FP4X4),
+                        ke_banks[u][:, c, b:b + step], lhsT=wk_codes[:, a, 2 * P * nt:2 * P * (nt + 1)].bitcast(FP4X4),
                         lhsT_scale=wk_scale_rows[:, a, P * nt:P * (nt + 1)],
                         rhs=x_codes[:, cols].bitcast(FP8X4), rhs_scale=x_scales[:, cols],
                         start=(a == 0 and c == 0 and b == 0),
@@ -224,24 +220,27 @@ def tile_list_hway_kernel(tc, xT, wgt, wk_words, wk_scales, wv, bg, res, offs, o
             for a in range(PASSES):
                 ve_pass(u, a)
 
+        rests = {}
         gated = {}
 
-        def open_unit(u, engines):
+        def open_unit(u):
             nt0, count, j0, width = UNITS[u]
-            rest = work.tile([P, count, width], F32, name="rest")
+            rests[u] = work.tile([P, count, width], F32, name="rest")
             gated[u] = work.tile([P, count, width], F32, name="gated")
             for c in range(count):
-                nc.scalar.activation(rest[:, c, :], ke_banks[u][:, c, :], ACT.Sigmoid,
+                nc.scalar.activation(rests[u][:, c, :], ke_banks[u][:, c, :], ACT.Sigmoid,
                                      bias=minus_bias[:, nt0 + c:nt0 + c + 1], scale=-1.0)
             nc.vector.tensor_tensor(gated[u][:], ve_banks[u][:], res_sb[u][:], ALU.subtract)
-            step = width // len(engines)
-            for place, engine in enumerate(engines):
-                cols = slice(place * step, (place + 1) * step)
-                engine.tensor_tensor(gated[u][:, :, cols], gated[u][:, :, cols], rest[:, :, cols], ALU.mult)
 
-        def close_unit(u, c0, width):
+        def multiply(u, engine, tag=None):
+            difference = gated[u]
+            if tag:
+                gated[u] = keep.tile([P, UNITS[u][1], UNITS[u][3]], F32, name="product%d" % u, tag=tag, align_bytes=64)
+            engine.tensor_tensor(gated[u][:], difference[:], rests[u][:], ALU.mult)
+
+        def close_unit(u, c0, width, tag):
             cols = slice(c0, c0 + width)
-            result = keep.tile([P, UNITS[u][1], width], F32, name="result%d_%d" % (u, c0))
+            result = keep.tile([P, UNITS[u][1], width], F32, name="result%d_%d" % (u, c0), tag=tag)
             nc.vector.tensor_tensor(result[:], ve_banks[u][:, :, cols], gated[u][:, :, cols], ALU.subtract)
             nc.sync.dma_start(unit_of(out, u)[:, :, cols], result[:])
 
@@ -258,9 +257,9 @@ def tile_list_hway_kernel(tc, xT, wgt, wk_words, wk_scales, wv, bg, res, offs, o
         xq[0, 0] = mx_operand("xg0_0", JH, "plane1_2")
         quantise_xg(rounded0[0][:], 0, 0, JH)
         for u in range(2):
-            ke_pass(u, 0)
-        for u in range(2):
             ve_pass(u, 0)
+        for u in range(2):
+            ke_pass(u, 0)
         rounded1 = keep.tile([P, J, PACK], BF16, name="rounded1", tag="wv_first0", align_bytes=64)
         round_pair(rounded1[:], 1, 0, 0, J)
         wv_first1_bf = round_wv_first(1)
@@ -290,17 +289,24 @@ def tile_list_hway_kernel(tc, xT, wgt, wk_words, wk_scales, wv, bg, res, offs, o
             finish_quarter(q)
 
         last = len(UNITS) - 1
-        open_unit(0, [nc.vector])
-        open_unit(1, [nc.gpsimd])
+        open_unit(0)
+        multiply(0, nc.vector)
+        open_unit(1)
+        multiply(1, nc.gpsimd)
         finish_quarter(J // JQ - 1)
         for u in range(2, len(UNITS)):
-            open_unit(u, [nc.vector, nc.gpsimd] if u == last else [nc.gpsimd])
-            close_unit(u - 2, 0, UNITS[u - 2][3])
+            open_unit(u)
+            if u < last:
+                multiply(u, nc.gpsimd)
+            else:
+                for engine, cols in ((nc.vector, slice(0, JQ)), (nc.gpsimd, slice(JQ, JH))):
+                    engine.tensor_tensor(gated[u][:, :, cols], gated[u][:, :, cols], rests[u][:, :, cols], ALU.mult)
+            close_unit(u - 2, 0, UNITS[u - 2][3], "result%d" % u)
             if u + 2 <= last:
                 nt = UNITS[u + 2][0]
                 if (0, nt) not in vq:
                     make_wv_second(nt)
                 all_passes(u + 2)
-        close_unit(last, 0, JQ)
-        close_unit(last - 1, 0, JH)
-        close_unit(last, JQ, JQ)
+        close_unit(last, 0, JQ, "result_a")
+        close_unit(last - 1, 0, JH, "result_b")
+        close_unit(last, JQ, JQ, "result_c")

from contextlib import ExitStack

import concourse.mybir as mybir
from concourse.masks import make_identity

K, N, T, J = 1024, 512, 2048, 1024
HEADS = 8
FLOPS = 2 * 2 * K * N * J
BYTES = 4 * K * T + 4 * HEADS * J + K * N // 2 + K * N // 32 + 4 * K * N + 4 * N + 4 * N * J + 2 * HEADS * J + 4 * N * J

F32 = mybir.dt.float32
BF16 = mybir.dt.bfloat16
I32 = mybir.dt.int32
U32 = mybir.dt.uint32
U16 = mybir.dt.uint16
U8 = mybir.dt.uint8
FP8X4 = mybir.dt.float8_e4m3fn_x4
FP4X4 = mybir.dt.float4_e2m1fn_x4
ALU = mybir.AluOpType
ACT = mybir.ActivationFunctionType

P = 128
QUAD = 32
GROUP = 16
PACK = 4
RUN = 4
SCALE_ROWS = 4
K_PASS = P * PACK
PASSES = K // K_PASS
JH = 512
JQ = 256
NH = 256
N_TILES = N // P

UNITS = [(0, 2, q * JQ, JQ) for q in range(J // JQ)] + [(nt, 1, h * JH, JH) for nt in (2, 3) for h in range(2)]
KE_BANK = [0, 1, 2, 7, 0, 2, 7, 0]
VE_BANK = [3, 4, 5, 6, 1, 3, 4, 5]


def tile_list_hway_kernel(tc, xT, wgt, wk_words, wk_scales, wv, bg, res, offs, out):
    nc = tc.nc
    with ExitStack() as ctx:
        keep = ctx.enter_context(tc.tile_pool(name="keep", bufs=1))
        work = ctx.enter_context(tc.tile_pool(name="work", bufs=J // JQ))
        psum = ctx.enter_context(tc.psum_pool(name="psum", bufs=1))

        def bank(shape, number):
            return psum.tile(shape, F32, name="bank%d" % number)

        offsets = keep.tile([P, J // GROUP], U16, name="offsets")
        weights = keep.tile([P, J], F32, name="weights", align_bytes=64)
        planes = [[keep.tile([P, T], F32, name="plane%d_%d" % (a, i), align_bytes=64) for i in range(PACK)]
                  for a in range(PASSES)]
        wk_codes = keep.tile([P, PASSES, 2 * N], U8, name="wk_codes", align_bytes=64)
        wk_scale_rows = keep.tile([P, PASSES, N], U8, name="wk_scale_rows", align_bytes=64)
        wv_first = [keep.tile([P, PACK, NH], F32, name="wv_first%d" % a, align_bytes=64) for a in range(PASSES)]
        wv_second = [keep.tile([P, PACK, NH], F32, name="wv_second%d" % a, align_bytes=64) for a in range(PASSES)]
        res_sb = [keep.tile([P, unit[1], unit[3]], F32, name="res%d" % u) for u, unit in enumerate(UNITS)]

        bias_rows = keep.tile([P, P], F32, name="bias_rows")
        identity = keep.tile([P, P], F32, name="identity")
        make_identity(nc, identity[:])
        nc.vector.memset(bias_rows[:], 0.0)
        nc.scalar.activation(bias_rows[:], bias_rows[:], ACT.Sigmoid)
        nc.vector.memset(wk_scale_rows[:].rearrange("p a n -> p (a n)").bitcast(I32), 0)

        def rows_of_pass(matrix, a):
            return matrix[a * K_PASS:(a + 1) * K_PASS, :].rearrange("(p i) c -> p i c", i=PACK)

        def load_plane(a, i):
            nc.sync.dma_start(planes[a][i][:], rows_of_pass(xT, a)[:, i, :])

        def load_wv_first(a):
            nc.sync.dma_start(wv_first[a][:], rows_of_pass(wv, a)[:, :, :NH])

        def load_wv_second(a):
            nc.sync.dma_start(wv_second[a][:], rows_of_pass(wv, a)[:, :, NH:])

        def unit_of(matrix, u):
            nt0, count, j0, width = UNITS[u]
            return matrix[nt0 * P:(nt0 + count) * P, j0:j0 + width].rearrange("(c p) j -> p c j", p=P)

        def load_res(u):
            nc.sync.dma_start(res_sb[u][:], unit_of(res, u))

        w_rows = keep.tile([P, 2, QUAD], F32, name="w_rows", align_bytes=64)
        w_turned = keep.tile([P, 2, 2, GROUP], F32, name="w_turned", align_bytes=64)
        w_spread = keep.tile([P, GROUP, 2, 2, GROUP], F32, name="w_spread", align_bytes=64)
        nc.sync.dma_start(w_rows[:].rearrange("p e s -> p (e s)"),
                          wgt[0:P:GROUP, :].rearrange("h (b c) -> h b c", b=GROUP))
        load_plane(0, 0)
        nc.sync.dma_start(offsets[:], offs)
        for e in range(2):
            nc.vector.transpose(w_turned[:, e, :, :].rearrange("p g b -> p (g b)"), w_rows[:, e, :])
        half_blocks = GROUP // 2
        for h in range(2):
            b = slice(half_blocks * h, half_blocks * (h + 1))
            nc.vector.tensor_copy(
                w_spread[:, b, :, :, :],
                w_turned[:, :, :, b].rearrange("p e g b -> p b e g").unsqueeze(4).to_broadcast([P, half_blocks, 2, 2, GROUP]))
        for h in range(2):
            b = slice(half_blocks * h, half_blocks * (h + 1))
            nc.vector.transpose(weights[:, h * JH:(h + 1) * JH],
                                w_spread[:, b, :, :, :].rearrange("p b e g r -> p (b e g r)"))

        for i in range(1, PACK):
            load_plane(0, i)
        for q in range(P // QUAD):
            nc.sync.dma_start(
                wk_scale_rows[QUAD * q:QUAD * q + SCALE_ROWS, :, :].bitcast(I32),
                wk_scales[:, SCALE_ROWS * q:SCALE_ROWS * (q + 1), :].rearrange("a r n -> r a n").bitcast(I32),
            )
        nc.sync.dma_start(bias_rows[0:N_TILES, :], bg.rearrange("(c p) -> c p", p=P))
        load_plane(1, 0)
        load_plane(1, 1)
        load_wv_first(0)
        load_plane(1, 2)
        load_wv_first(1)
        load_plane(1, 3)
        nc.sync.dma_start(wk_codes[:].bitcast(I32), wk_words.rearrange("a p n -> p a n").bitcast(I32))
        load_res(0)
        load_res(1)
        load_wv_second(0)
        load_wv_second(1)
        for u in range(2, len(UNITS)):
            load_res(u)

        minus_bias = keep.tile([P, N_TILES], F32, name="minus_bias")
        bias_turned = bank([P, P], KE_BANK[0])
        nc.tensor.transpose(bias_turned[:], bias_rows[:], identity[:])
        nc.scalar.mul(minus_bias[:], bias_turned[:, 0:N_TILES], -1.0)

        picked = [keep.tile([P, PACK, J], F32, name="picked%d" % a) for a in range(PASSES)]
        xq = {}
        vq = {}

        def mx_operand(name, width, tag):
            codes = keep.tile([P, width], U32, name=name + "_codes", tag=tag, align_bytes=64)
            scales = keep.tile([P, width], U8, name=name + "_scales", align_bytes=64)
            return codes[:], scales[:]

        def gather(a, i, j0, width):
            nc.vector.tensor_tensor(
                picked[a][:, i, j0:j0 + width],
                planes[a][i][:].indirect(offsets[:, j0 // GROUP:(j0 + width) // GROUP]),
                weights[:, j0:j0 + width],
                ALU.mult,
            )

        def round_pair(rounded, a, i0, j0, width):
            nc.scalar.copy(rounded[:, :, i0:i0 + 2], picked[a][:, i0:i0 + 2, j0:j0 + width].rearrange("p i w -> p w i"))

        def quantise_xg(rounded, a, j0, width):
            codes, scales = xq[a, j0 // JH]
            c0 = j0 % JH
            nc.vector.quantize_mx(codes[:, c0:c0 + width].bitcast(FP8X4), scales[:, c0:c0 + width],
                                  rounded.rearrange("p w i -> p (w i)"))

        def round_wv(rounded, rows):
            nc.scalar.copy(rounded.rearrange("p (c r) i -> p c i r", r=RUN), rows.rearrange("p i (c r) -> p c i r", r=RUN))

        def round_wv_first(a):
            rounded = keep.tile([P, NH, PACK], BF16, name="wv_first_bf%d" % a, align_bytes=64)
            round_wv(rounded[:], wv_first[a][:])
            return rounded

        def quantise_wv_first(rounded, a, tag):
            codes, scales = mx_operand("wv_first%d" % a, NH, tag)
            nc.vector.quantize_mx(codes.bitcast(FP8X4), scales, rounded[:].rearrange("p n i -> p (n i)"))
            for nt in range(NH // P):
                vq[a, nt] = (codes[:, nt * P:(nt + 1) * P], scales[:, nt * P:(nt + 1) * P])

        def make_wv_second(nt):
            c0 = nt * P - NH
            rounded = keep.tile([P, PASSES, P, PACK], BF16, name="wv_second_bf%d" % nt, align_bytes=64)
            for a in range(PASSES):
                round_wv(rounded[:, a, :, :], wv_second[a][:, :, c0:c0 + P])
            codes, scales = mx_operand("wv_second%d" % nt, PASSES * P, "wv_second%d_codes" % nt)
            nc.vector.quantize_mx(codes.bitcast(FP8X4), scales, rounded[:].rearrange("p a n i -> p (a n i)"))
            for a in range(PASSES):
                vq[a, nt] = (codes[:, a * P:(a + 1) * P], scales[:, a * P:(a + 1) * P])

        ke_banks = {}
        ve_banks = {}

        def ke_pass(u, a):
            nt0, count, j0, width = UNITS[u]
            if a == 0:
                ke_banks[u] = bank([P, count, width], KE_BANK[u])
            x_codes, x_scales = xq[a, j0 // JH]
            c0 = j0 % JH
            step = width
            for c in range(count):
                nt = nt0 + c
                for b in range(0, width, step):
                    cols = slice(c0 + b, c0 + b + step)
                    nc.tensor.matmul_mx(
                        ke_banks[u][:, c, b:b + step], lhsT=wk_codes[:, a, 2 * P * nt:2 * P * (nt + 1)].bitcast(FP4X4),
                        lhsT_scale=wk_scale_rows[:, a, P * nt:P * (nt + 1)],
                        rhs=x_codes[:, cols].bitcast(FP8X4), rhs_scale=x_scales[:, cols],
                        start=(a == 0 and c == 0 and b == 0),
                        stop=(a == PASSES - 1 and c == count - 1 and b + step == width))

        def ve_pass(u, a):
            nt0, count, j0, width = UNITS[u]
            if a == 0:
                ve_banks[u] = bank([P, count, width], VE_BANK[u])
            x_codes, x_scales = xq[a, j0 // JH]
            cols = slice(j0 % JH, j0 % JH + width)
            for c in range(count):
                v_codes, v_scales = vq[a, nt0 + c]
                nc.tensor.matmul_mx(
                    ve_banks[u][:, c, :], lhsT=v_codes.bitcast(FP8X4), lhsT_scale=v_scales,
                    rhs=x_codes[:, cols].bitcast(FP8X4), rhs_scale=x_scales[:, cols],
                    start=(a == 0 and c == 0), stop=(a == PASSES - 1 and c == count - 1))

        def all_passes(u):
            for a in range(PASSES):
                ke_pass(u, a)
            for a in range(PASSES):
                ve_pass(u, a)

        rests = {}
        gated = {}

        def open_unit(u):
            nt0, count, j0, width = UNITS[u]
            rests[u] = work.tile([P, count, width], F32, name="rest")
            gated[u] = work.tile([P, count, width], F32, name="gated")
            for c in range(count):
                nc.scalar.activation(rests[u][:, c, :], ke_banks[u][:, c, :], ACT.Sigmoid,
                                     bias=minus_bias[:, nt0 + c:nt0 + c + 1], scale=-1.0)
            nc.vector.tensor_tensor(gated[u][:], ve_banks[u][:], res_sb[u][:], ALU.subtract)

        def multiply(u, engine, tag=None):
            difference = gated[u]
            if tag:
                gated[u] = keep.tile([P, UNITS[u][1], UNITS[u][3]], F32, name="product%d" % u, tag=tag, align_bytes=64)
            engine.tensor_tensor(gated[u][:], difference[:], rests[u][:], ALU.mult)

        def close_unit(u, c0, width, tag):
            cols = slice(c0, c0 + width)
            result = keep.tile([P, UNITS[u][1], width], F32, name="result%d_%d" % (u, c0), tag=tag)
            nc.vector.tensor_tensor(result[:], ve_banks[u][:, :, cols], gated[u][:, :, cols], ALU.subtract)
            nc.sync.dma_start(unit_of(out, u)[:, :, cols], result[:])

        rounded0 = [keep.tile([P, JH, PACK], BF16, name="rounded0_%d" % h, align_bytes=64) for h in range(2)]
        for i in range(PACK):
            gather(0, i, 0, J)
            if i % 2 == 1:
                for h in range(2):
                    round_pair(rounded0[h][:], 0, i - 1, h * JH, JH)
        gather(1, 0, 0, J)
        gather(1, 1, 0, J)
        quantise_wv_first(round_wv_first(0), 0, "wv_first0_codes")
        gather(1, 2, 0, J)
        xq[0, 0] = mx_operand("xg0_0", JH, "plane1_2")
        quantise_xg(rounded0[0][:], 0, 0, JH)
        for u in range(2):
            ve_pass(u, 0)
        for u in range(2):
            ke_pass(u, 0)
        rounded1 = keep.tile([P, J, PACK], BF16, name="rounded1", tag="wv_first0", align_bytes=64)
        round_pair(rounded1[:], 1, 0, 0, J)
        wv_first1_bf = round_wv_first(1)
        for h in range(2):
            xq[1, h] = mx_operand("xg1_%d" % h, JH, "xg1_%d_codes" % h)

        gather(1, PACK - 1, 0, JQ)
        gather(1, PACK - 1, JQ, JQ)
        gather(1, PACK - 1, JH, JH)

        def finish_quarter(q):
            piece = rounded1[:, q * JQ:(q + 1) * JQ, :]
            round_pair(piece, 1, 2, q * JQ, JQ)
            quantise_xg(piece, 1, q * JQ, JQ)
            if q == 0:
                quantise_wv_first(wv_first1_bf, 1, "plane1_3")
            if q == 1:
                xq[0, 1] = mx_operand("xg0_1", JH, "wv_first_bf1")
                quantise_xg(rounded0[1][:], 0, JH, JH)
            if q * JQ < JH:
                ke_pass(q, 1)
                ve_pass(q, 1)
            else:
                all_passes(q)

        for q in range(J // JQ - 1):
            finish_quarter(q)

        last = len(UNITS) - 1
        open_unit(0)
        multiply(0, nc.vector)
        open_unit(1)
        multiply(1, nc.gpsimd)
        finish_quarter(J // JQ - 1)
        for u in range(2, len(UNITS)):
            open_unit(u)
            if u < last:
                multiply(u, nc.gpsimd)
            else:
                for engine, cols in ((nc.vector, slice(0, JQ)), (nc.gpsimd, slice(JQ, JH))):
                    engine.tensor_tensor(gated[u][:, :, cols], gated[u][:, :, cols], rests[u][:, :, cols], ALU.mult)
            close_unit(u - 2, 0, UNITS[u - 2][3], "result%d" % u)
            if u + 2 <= last:
                nt = UNITS[u + 2][0]
                if (0, nt) not in vq:
                    make_wv_second(nt)
                all_passes(u + 2)
        close_unit(last, 0, JQ, "result_a")
        close_unit(last - 1, 0, JH, "result_b")
        close_unit(last, JQ, JQ, "result_c")
